import numpy as np, ml_dtypes
CORES = [2,6,10,14,18,22,26,30]
N = 8
import mx_ref
BF = ml_dtypes.bfloat16
def gentries(a):
    return np.ascontiguousarray(a.reshape(8, 16, -1).transpose(0, 2, 1)).reshape(8, -1)
def gtable(e):
    e = np.asarray(e); return np.ascontiguousarray(e.reshape(8, -1, 16).transpose(0, 2, 1)).reshape(128, -1).astype(np.int32)
def gcols(t, e):
    v = np.concatenate([t.reshape(8, 16, -1, 4), np.zeros((8, 16, 1, 4), BF)], axis=2)
    return np.ascontiguousarray(np.stack([v[g][:, e[g]] for g in range(8)])).reshape(128, -1)
def tile(rs):
    return np.stack(rs, axis=2).reshape(128, -1).astype(BF)
def pick(q, e):
    c = np.concatenate([q[0].reshape(128, -1, 4), np.zeros((128, 1, 4), np.uint8)], axis=1); s = np.concatenate([q[1], np.ones((16, 1), np.uint8)], axis=1)
    return (np.ascontiguousarray(c[:, e].reshape(128, -1)), np.ascontiguousarray(s[:, e]))
def join(*qs):
    return (np.concatenate([q[0] for q in qs], axis=1), np.concatenate([q[1] for q in qs], axis=1))
def put(q, e, v):
    c, s = q[0].reshape(128, -1, 4).copy(), q[1].copy(); c[:, e] = v[0].reshape(128, -1, 4); s[:, e] = v[1]
    return (c.reshape(128, -1), s)
def pk(c, s):
    return (np.ascontiguousarray(c), mx_ref.live(s))
def emit(q):
    return q[0], q[1]
def packed(v, rng):
    q = [mx_ref.quantize(np.ascontiguousarray(v[r])) for r in range(N)]
    return np.stack([a for a, b in q]), np.stack([mx_ref.plane(b, rng) for a, b in q])
def values_of_codes():
    e, c = np.zeros((128, 128, 4), np.float32), np.zeros((128, 2, 4), np.uint8)
    e[np.arange(128), np.arange(128), 0] = 1
    c[:127, :, 0] = np.arange(256).reshape(2, 128).T[:127]
    return mx_ref.matmul(mx_ref.quantize(e.reshape(128, 512).astype(BF)), (c.reshape(128, 8), np.full((16, 2), 127, np.uint8))).T.reshape(-1).astype(np.float64)
CODE_VALUE, SCALE_VALUE = values_of_codes(), 2.0 ** (np.arange(256) - 127.0)
def decode(q):
    return (CODE_VALUE[q[0]].reshape(16, 8, -1, 4) * SCALE_VALUE[q[1]][:, None, :, None] + 0.0).reshape(128, -1).astype(np.float32)
def f(rng, *shape):
    return mx_ref.flush((rng.standard_normal(shape, dtype=np.float32) * np.exp2(rng.integers(-2, 3, shape[:-1] + (1,)))).astype(BF))
def wide(rng, *shape, cols=0):
    v = rng.standard_normal(shape, dtype=np.float32) * np.exp2(rng.integers(-12, 13, shape)).astype(np.float32)
    if cols: v *= np.repeat(np.exp2(rng.integers(-cols, cols + 1, shape[:-2] + (1, shape[-1] // 4))) * (rng.random(shape[:-2] + (1, shape[-1] // 4)) > 0.0625), 4, axis=-1).astype(np.float32)
    return mx_ref.flush(v.astype(BF))
C, HALF = 320, 160
MASK = [1, 2, 4]
def numbers_of(rng):
    return {"x": np.array(f(rng, N, 128, 4 * C)), "u": np.array(f(rng, N, 128, 512)), "v": np.array(f(rng, N, 128, 512))}
def orders(rng):
    e = np.tile(np.arange(C), (N, 8, 1))
    k = [rng.permuted(e, axis=2) for i in range(4)]
    t = np.zeros((N, 8, C), np.int64)
    np.put_along_axis(t, k[3], np.ascontiguousarray(k[3].reshape(N, 8, HALF, 2)[:, :, :, ::-1]).reshape(N, 8, C), axis=2)
    return k[:3] + [t]
def stored(k):
    return {n: np.stack([gtable(a[r]) for r in range(N)]) for n, a in zip(("lg", "pb", "fd", "ex"), k)}
def lists(rng):
    return stored(orders(rng))
def layers(rng):
    return np.array(f(rng, N, 128, 2048)).reshape(N, 8, 16, 4, 8, 16, 4)
def weights(rng, w):
    c, p = packed(np.ascontiguousarray(w).reshape(N, 128, 2048), rng)
    return {"wc": c, "ws": p}
def setup_inputs(rng):
    return {**numbers_of(rng), **lists(rng), **weights(rng, layers(rng))}
def setup_inputs_ties(rng):
    d = numbers_of(rng)
    o = rng.permutation(N)
    k = rng.integers(-1, 2, (N, 8, 4, C)).astype(np.float32)
    k[o[1]] = 1
    k[o[2]] = -1
    x = d["x"].reshape(N, 8, 16, C, 4)
    x[:, :, :4] = 0
    x[:, :, :4, :, 0] = k.astype(BF)
    u = d["u"].reshape(N, 8, 16, 8, 16, 4)
    u[:, :, :, :, :4] = 0
    for g in range(8):
        for j in range(4): u[:, g, j, g, j, 0] = 1.0
    u[o[0], :, :, :, :4] = 0
    w = layers(rng)
    w[:, :, :, :, :, :4] = 0
    return {"x": x.reshape(N, 128, 4 * C), "u": u.reshape(N, 128, 512), "v": d["v"], **lists(rng), **weights(rng, w)}
def setup_inputs_near(rng):
    d = numbers_of(rng)
    o = rng.permutation(N)
    k = np.ones(N, np.float32)
    k[o[:N // 2]] = 2.0 ** -30
    s = rng.integers(-1, 2, (N, 8, 4, C)) * np.where(k < 1, 2 * k, k)[:, None, None, None]
    x = d["x"].astype(np.float32).reshape(N, 8, 16, C, 4)
    x[:, :, :8] = 0
    x[:, :, 0:8:2, :, 0] = 1.125 * s
    x[:, :, 1:8:2, :, 0] = -1.25 * s
    for r in range(N):
        at_ = [0, C - 1, int(rng.integers(C)), int(rng.integers(C))]
        for g, c in zip(rng.permutation(8)[:4], at_): x[r, g, 2 * rng.integers(4), c, 0] = 2.0 ** 30 * rng.choice([-1.0, 1.0])
    x[o[0], :, 8:] = 0
    x[o[0], :, 12:, :, 0] = rng.choice([-1.0, 1.0], (8, 4, C)) * 2.0 ** -30
    x[o[0], :, 12, :, 2] = 2.0 ** -30
    u = d["u"].reshape(N, 8, 16, 8, 16, 4)
    u[:, :, :, :, :4] = 0
    w = np.zeros((N, 8, 16, 4, 8, 16, 4), np.float32)
    for g in range(8):
        for j in range(4):
            u[:, g, 2 * j, g, j, 0] = (1.125 * k).astype(np.float32).astype(BF)
            u[:, g, 2 * j + 1, g, j, 0] = k.astype(BF)
            w[:, g, 12 + j, 0, g, 8 + j, 0] = 1.125 * 2.0 ** -8
            w[:, g, 12 + j, 1, g, 8 + (j + 1) % 4, 0] = -1.25 * 2.0 ** -8
        w[:, g, 12, 1, g, 12, 2] = 2.0 ** 5
    u[o[0], :, :, :, :4] = 0
    for g in range(8):
        for j in range(4):
            u[o[0], g, 8 + j, g, j, 0] = 1.125 * 2.0 ** -30
            u[o[0], g, 8 + (j + 1) % 4, g, j, 1] = 2.0 ** -30
    return {"x": x.reshape(N, 128, 4 * C).astype(BF), "u": u.reshape(N, 128, 512), "v": d["v"], **lists(rng), **weights(rng, w.astype(BF))}
def setup_inputs_odd(rng):
    d = numbers_of(rng)
    x = np.zeros((N, 8, 16, C, 4), np.float32)
    x[:, :, 0, :, 1] = 1.96875 * 2.0 ** 8 * rng.choice([-1.0, 1.0], (N, 8, C))
    x[:, :, :4, :, 0] = -(8 + rng.integers(0, 2, (N, 8, 4, C))) * 2.0 ** -8
    x[:, :, 4:8, :, 0] = 8 * 2.0 ** -8
    a = np.exp2(rng.integers(-3, 4, 8).astype(np.float32))[None, :, None]
    x[:, :, 8, :, 0] = -2.953125 * a
    x[:, :, 12, :, 0] = -1.125 * a
    x[:, :, 14, :, 0] = -0.0703125 * a
    u = d["u"].reshape(N, 8, 16, 8, 16, 4)
    u[:, :, :, :, :4] = 0
    w = np.zeros((N, 8, 16, 4, 8, 16, 4), np.float32)
    for g in range(8):
        for j in range(4):
            u[:, g, j, g, j, 0] = 1.0
            u[:, g, 4 + j, g, j, 0] = 1.0
            w[:, g, 14, j, g, 9, 0] = -2.0 ** (j - 5)
        w[:, g, 12, 0, g, 8, 0] = -28.0
    return {"x": x.reshape(N, 128, 4 * C).astype(BF), "u": u.reshape(N, 128, 512), "v": d["v"], **lists(rng), **weights(rng, w.astype(BF))}
def setup_inputs_ends(rng):
    d = numbers_of(rng)
    o, e = rng.permutation(N) % 4, rng.permutation(N) % 4
    s = rng.choice([-1.0, 1.0], (N, 128, C, 4))
    s[o == 0] = -1
    s[o == 1] = rng.choice([-1.0, 1.0], (N, 1, C, 1))[o == 1]
    for r in range(N):
        if o[r] == 3: s[r, ::8, :, 0] = 1
    x = s * (0.955 + 0.02 * rng.random((N, 128, C, 4))) * 2.0 ** 30
    x[o == 3] = s[o == 3] * 2.0 ** -30
    size = np.where(o == 3, 2.0 ** -30, 2.0 ** 30)
    a = np.stack([rng.permutation(32).reshape(8, 4) % 2 * 2.0 - 1.0 for r in range(N)]) * size[:, None, None]
    u = d["u"].reshape(N, 128, 8, 16, 4)
    u[:, :, :, :4] = a.astype(np.float32).astype(BF)[:, None, :, :, None]
    v = rng.choice([-1.0, 1.0], (N, 128, 512)) * size[:, None, None]
    c = np.arange(C)
    plain, pairs = [c, c[::-1], (c + 1) % C], [c[::-1], c ^ 1, (c + HALF) % C]
    k = orders(rng)
    for r in range(N):
        if e[r] < 3:
            for n in range(3): k[n][r] = plain[(e[r] + n) % 3]
            k[3][r] = pairs[e[r]]
    h = np.where(o == 3, 32.0, -0.125)[:, None] * np.ones((1, 128))
    for r in range(N):
        if o[r] == 3:
            h[r, 14::16] = 2.0 ** -8
            h[r, 15::16] = 2.0 ** 8
        else: h[r, 15::16] = 0
    w = np.zeros((N, 128, 4, 128, 4), np.float32)
    i = np.arange(128)
    for b in range(4): w[:, i, b, i, b] = h
    return {"x": x.astype(np.float32).reshape(N, 128, 4 * C).astype(BF), "u": u.reshape(N, 128, 512), "v": v.astype(np.float32).astype(BF), **stored(k), **weights(rng, w.astype(BF))}
def setup_inputs_spread(rng):
    d = setup_inputs(rng)
    d["x"] = wide(rng, N, 128, 4 * C, cols=6)
    return d
def check_inputs(d):
    b = []
    for k in ("x", "u", "v"):
        a = np.abs(d[k].astype(np.float32))
        if not (np.isfinite(a).all() and ((a == 0) | (a >= 2.0 ** -30) & (a <= 2.0 ** 30)).all()): b.append("a value of " + k)
    for k in ("lg", "pb", "fd"):
        if not (np.sort(d[k].reshape(N, 8, C), axis=2) == np.arange(C)).all(): b.append(k + ": no permutation")
    for r in range(N):
        e = gentries(d["ex"][r])
        if not ((e >= 0) & (e < C)).all(): b.append("an entry of ex")
        elif (e == np.arange(C)).any() or (at(e, e) != np.arange(C)).any(): b.append("ex: no pairs")
    none, least, most = [emit(mx_ref.quantize(np.full((128, 16), k, np.float32).astype(BF)))[1][0, 0] for k in (0.0, 2.0 ** -8, 2.0 ** 8)]
    for r in range(N):
        if ((d["wc"][r] == 0x7F) | (d["wc"][r] == 0xFF)).any(): b.append("wc: a code that is no number")
        s = mx_ref.live(d["ws"][r])
        if ((s != none) & ((s < least) | (s > most))).any(): b.append("ws: a scale out of range")
        if (((d["wc"][r].reshape(16, 8, 512, 4) & 0x7F) != 0) & (s == none)[:, None, :, None]).any(): b.append("wc: a code other than zero under the scale of zeros")
    return b
def at(t, e):
    return np.take_along_axis(t, e.astype(np.int64), axis=1)
def reference(x, u, v, lg, pb, fd, ex, wc, ws):
    qu = [mx_ref.quantize(u[r]) for r in range(N)]
    lay = [pk(wc[r], ws[r]) for r in range(N)]
    leg, back, fore, pair = [[gentries(t[r]) for r in range(N)] for t in (lg, pb, fd, ex)]
    now = [x[r] for r in range(N)]
    for mask in MASK:
        made, swapped = [], []
        for r in range(N):
            s = mx_ref.matmul(qu[r], mx_ref.quantize(now[r])).reshape(8, 16, C)
            low = np.minimum(np.arange(C), pair[r])
            turn = [np.where(at(s[:, j], low) < 0, pair[r], np.arange(C)) for j in range(4)]
            for j, b in enumerate((back[r ^ mask], back[r], back[r ^ mask])):
                leg[r] = at(b, at(turn[j], at(leg[r], fore[r])))
            swapped.append(at(back[r], turn[3]))
            z = (gcols(now[r], leg[r]).astype(np.float32) + gcols(now[r], at(leg[r], fore[r])).astype(np.float32)) * np.float32(0.5)
            q = mx_ref.quantize(z.astype(BF))
            made.append(tile([mx_ref.matmul(pick(lay[r], np.arange(128 * b, 128 * b + 128)), q) * np.float32(0.03125) for b in range(4)]))
        new = []
        for r in range(N):
            m = at(fore[r], leg[r])
            far = gcols(decode(mx_ref.quantize(made[r ^ mask])).astype(BF), m[:, :HALF])
            near = gcols(made[r], m[:, HALF:])
            new.append((now[r].astype(np.float32) + np.concatenate([far, near], axis=1).astype(np.float32)).astype(BF))
        now, back = new, swapped
    y, pl = np.zeros((N, 128, C), np.float32), np.zeros((N, 8, 2 * C), np.float32)
    oc, osc = np.zeros((N, 128, 4 * C), np.uint8), np.zeros((N, 16, C), np.uint8)
    for r in range(N):
        q = mx_ref.quantize(now[r])
        y[r] = mx_ref.matmul(mx_ref.quantize(v[r]), q)
        pl[r] = np.concatenate([leg[r], back[r]], axis=1)
        oc[r], osc[r] = emit(q)
    return {"y": y, "pl": pl, "oc": oc, "osc": osc}

@@ -1,0 +1,467 @@
+from concourse.mybir import dt, AluOpType, ActivationFunctionType
+
+C, HALF = 320, 160
+MASKS = (1, 2, 4)
+PIECES = ((0, 192), (192, 320))
+
+SCRATCH = {
+    "xi": ("sbuf", [128, 4 * C], "bfloat16"), "xg": ("sbuf", [128, 4 * C], "bfloat16"),
+    "ag": ("sbuf", [128, 4 * C], "bfloat16"), "zt": ("sbuf", [128, 4 * C], "bfloat16"),
+    "hg": ("sbuf", [128, 4 * C], "bfloat16"), "hf": ("sbuf", [128, 4 * HALF], "bfloat16"),
+    "ut": ("sbuf", [128, 512], "bfloat16"), "vt": ("sbuf", [128, 512], "bfloat16"),
+    "ones": ("sbuf", [128, 512], "bfloat16"), "et": ("sbuf", [128, 2048], "bfloat16"),
+    "uq": ("sbuf", [128, 128], "float8_e4m3fn_x4"), "us": ("sbuf", [128, 128], "uint8"),
+    "vq": ("sbuf", [128, 128], "float8_e4m3fn_x4"), "vs": ("sbuf", [128, 128], "uint8"),
+    "wq": ("sbuf", [128, 512], "float8_e4m3fn_x4"), "wp": ("sbuf", [128, 512], "uint8"),
+    "eq": ("sbuf", [128, 512], "float8_e4m3fn_x4"), "es": ("sbuf", [128, 512], "uint8"),
+    "xq": ("sbuf", [128, C], "float8_e4m3fn_x4"), "xs": ("sbuf", [128, C], "uint8"),
+    "zq": ("sbuf", [128, C], "float8_e4m3fn_x4"), "zs": ("sbuf", [128, C], "uint8"),
+    "iY": ("sbuf", [128, 20], "int32"), "iP": ("sbuf", [128, 20], "int32"),
+    "iF": ("sbuf", [128, 20], "int32"), "iE": ("sbuf", [128, 20], "int32"),
+    "uY": ("sbuf", [128, 32], "uint16"), "uP": ("sbuf", [128, 32], "uint16"),
+    "uF": ("sbuf", [128, 32], "uint16"), "uE": ("sbuf", [128, 32], "uint16"),
+    "uM": ("sbuf", [128, 32], "uint16"), "uR": ("sbuf", [128, 32], "uint16"),
+    "off": ("sbuf", [128, 16], "uint16"),
+    "ip": ("sbuf", [128, 20], "int32"), "ik": ("sbuf", [128, 20], "int32"),
+    "i16": ("sbuf", [128, 20], "int32"), "cw": ("sbuf", [128, 20], "int32"), "iM": ("sbuf", [128, 20], "int32"),
+    "o1": ("sbuf", [128, 8], "int32"), "o2": ("sbuf", [128, 8], "int32"), "o3": ("sbuf", [128, 8], "int32"),
+    "o4": ("sbuf", [128, 8], "int32"),
+    "f1": ("sbuf", [128, 8], "float32"), "f2": ("sbuf", [128, 8], "float32"), "f3": ("sbuf", [128, 8], "float32"),
+    "f4": ("sbuf", [128, 8], "float32"), "f5": ("sbuf", [128, 8], "float32"),
+    "bs": ("sbuf", [128, 80], "float32"), "df": ("sbuf", [128, 80], "float32"),
+    "pr": ("sbuf", [128, 80], "float32"), "tb": ("sbuf", [128, 80], "float32"),
+    "pe": ("sbuf", [128, 32], "float32"), "t2": ("sbuf", [128, 32], "float32"),
+    "idn": ("sbuf", [128, C], "bfloat16"), "fm": ("sbuf", [128, C], "bfloat16"),
+    "wf": ("sbuf", [128, C], "bfloat16"), "pp": ("sbuf", [128, C], "bfloat16"), "po": ("sbuf", [128, C], "bfloat16"),
+    "sg": ("sbuf", [128, C], "bfloat16"), "g1": ("sbuf", [128, C], "bfloat16"), "g2": ("sbuf", [128, C], "bfloat16"),
+    "g3": ("sbuf", [128, C], "bfloat16"), "g4": ("sbuf", [128, C], "bfloat16"), "ya": ("sbuf", [128, C], "bfloat16"),
+    "yc": ("sbuf", [128, C], "bfloat16"), "yf": ("sbuf", [128, C + 32], "bfloat16"),
+    "nm": ("sbuf", [128, C + 32], "bfloat16"), "yb": ("sbuf", [128, C + 32], "bfloat16"),
+    "cb": ("sbuf", [128, C + 32], "bfloat16"), "cc": ("sbuf", [128, C + 32], "bfloat16"),
+    "idf": ("sbuf", [128, C], "float32"),
+    "tw2": ("sbuf", [128, 2 * C + 32], "bfloat16"), "tw0": ("sbuf", [128, 2 * C + 32], "bfloat16"), "tw1": ("sbuf", [128, 2 * C + 32], "bfloat16"),
+    "yo": ("sbuf", [128, C], "float32"), "pout": ("sbuf", [128, 2 * C], "float32"),
+    "lp1": ("sbuf", [128, 20], "int32"), "lp2": ("sbuf", [128, 20], "uint16"), "lp3": ("sbuf", [128, 20], "uint16"),
+    "psA": ("psum", [128, 2048], "float32"), "psB": ("psum", [128, 2048], "float32"),
+}
+for _r in "123":
+    SCRATCH["tu" + _r] = ("sbuf", [128, 80], "uint16")
+    SCRATCH["yk" + _r] = ("sbuf", [128, 48], "uint16")
+    SCRATCH["yg" + _r] = ("sbuf", [128, 32], "uint16")
+    SCRATCH["y3" + _r] = ("sbuf", [128, 32], "uint16")
+    SCRATCH["kl" + _r] = ("sbuf", [128, 16], "uint16")
+    SCRATCH["hq" + _r] = ("sbuf", [128, HALF], "float8_e4m3fn_x4")
+    SCRATCH["hs" + _r] = ("sbuf", [128, HALF], "uint8")
+    SCRATCH["lq" + _r] = ("sbuf", [128, HALF], "float8_e4m3fn_x4")
+    SCRATCH["ls" + _r] = ("sbuf", [128, HALF], "uint8")
+
+LOADS = ["d_pb", "d_ex", "d_fd", "d_lg", "d_x0", "d_x1", "d_u", "d_v", "d_wc", "d_ws", "d_wf"]
+ARRIVALS = ["a_%s%d" % (k, r) for k in "pkqs" for r in (1, 2, 3)]
+SEMAPHORES = ["c_v", "c_s", "c_t", "c_g", "sent", "stored"] + LOADS + ARRIVALS
+
+
+def rank_program(g, core, T, topo):
+    rank = T.rank_of(core)
+    if rank is None:
+        return
+    queue = {"v": g.vector, "s": g.scalar, "t": g.tensor, "g": g, "y": g.sync}
+    count = {"c_v": 0, "c_s": 0, "c_t": 0, "c_g": 0, "sent": 0, "stored": 0}
+    known = {q: {} for q in queue}
+    touched = {n: [] for n in SCRATCH}
+    copy = ActivationFunctionType.Copy
+    add, sub, mul, less = AluOpType.add, AluOpType.subtract, AluOpType.mult, AluOpType.is_lt
+
+    def meets(a, b):
+        if a[1] <= b[0] or b[1] <= a[0]:
+            return False
+        if a[2] == b[2]:
+            return (a[0] - b[0]) % a[2] == 0
+        return True
+
+    def order(q, reads, writes):
+        deps = []
+        for regs, w in ((reads, False), (writes, True)):
+            for n, a, b, st in regs:
+                for reg, wrote, op in touched[n]:
+                    if (w or wrote) and meets((a, b, st), reg) and known[q].get(op[0], 0) < op[1]:
+                        deps.append(op)
+        want = {}
+        for op in deps:
+            if any(o is not op and o[2].get(op[0], 0) >= op[1] and not (o[0] == op[0] and o[1] == op[1]) for o in deps):
+                continue
+            want[op[0]] = max(want.get(op[0], 0), op[1])
+        for s in want:
+            queue[q].wait_ge(T.sem[s], want[s])
+        for op in deps:
+            for s, c in op[2].items():
+                known[q][s] = max(known[q].get(s, 0), c)
+
+    def note(op, reads, writes):
+        for n, a, b, st in writes:
+            if st == 1:
+                touched[n][:] = [t for t in touched[n] if not (a <= t[0][0] and t[0][1] <= b)]
+            touched[n].append(((a, b, st), True, op))
+        for n, a, b, st in reads:
+            touched[n].append(((a, b, st), False, op))
+
+    def run(q, call, outs, ins):
+        reads = [r for v in ins for r in v[1]]
+        writes = [r for v in outs for r in v[1]]
+        order(q, reads, writes)
+        sem = "c_" + q
+        count[sem] += 1
+        call().then_inc(T.sem[sem], 1)
+        clock = dict(known[q])
+        clock[sem] = count[sem]
+        note((sem, count[sem], clock), reads, writes)
+
+    def V(n, a=0, b=None, st=1):
+        b = SCRATCH[n][1][1] if b is None else b
+        t = T[n]
+        if SCRATCH[n][0] == "psum":
+            return (t[:, a:b], [(n, 512 * (a // 512), 512 * (a // 512) + 512, 1)])
+        return (t[:, a:b:st] if st > 1 else t[:, a:b], [(n, a, b, st)])
+
+    def pick(win, off):
+        return (win[0].indirect(off[0]), win[1] + off[1])
+
+    def cp(q, out, in_, scale=None):
+        if q == "v":
+            run(q, lambda: g.vector.tensor_copy(out[0], in_[0]), [out], [in_])
+        elif scale is not None:
+            run(q, lambda: g.scalar.activation(out[0], in_[0], copy, scale=scale), [out], [in_])
+        else:
+            run(q, lambda: g.scalar.activation(out[0], in_[0], copy), [out], [in_])
+
+    def tt(out, a, b, op):
+        run("v", lambda: g.vector.tensor_tensor(out[0], a[0], b[0], op), [out], [a, b])
+
+    def ts(out, a, s1, op0, s2=None, op1=None):
+        cols = [s for s in (s1, s2) if isinstance(s, tuple)]
+        p1 = s1[0] if isinstance(s1, tuple) else s1
+        p2 = s2[0] if isinstance(s2, tuple) else s2
+        if op1 is None:
+            run("v", lambda: g.vector.tensor_scalar(out[0], a[0], p1, None, op0), [out], [a] + cols)
+        else:
+            run("v", lambda: g.vector.tensor_scalar(out[0], a[0], p1, p2, op0, op1), [out], [a] + cols)
+
+    def quant(q, s, t):
+        run("v", lambda: g.vector.quantize_mx(q[0], s[0], t[0]), [q, s], [t])
+
+    def mm(out, w, ws, x, xs):
+        run("t", lambda: g.tensor.matmul_mx(out[0], w[0], ws[0], x[0], xs[0], True, True), [out], [w, ws, x, xs])
+
+    def load(q, out, src, sem, codes=False):
+        order(q, [], out[1])
+        ap = out[0].bitcast(dt.uint8) if codes else out[0]
+        queue[q].dma_start(ap, src).then_inc(T.sem[sem], 16)
+        note((sem, 16, {sem: 16}), [], out[1])
+
+    def store(q, dst, src, regs):
+        order(q, regs, [])
+        queue[q].dma_start(dst, src).then_inc(T.sem.stored, 16)
+        count["stored"] += 16
+
+    def send(dst, out, in_, sem, lo, hi, codes=False):
+        order("g", in_[1], [])
+        es = topo.engines(core, dst)[lo:hi]
+        rid, pid, _ = topo.addr(dst)
+        o, i = (out[0].bitcast(dt.uint8), in_[0].bitcast(dt.uint8)) if codes else (out[0], in_[0])
+        g.remote_dma(o, i, T.sem[sem], T.sem.sent, pid, rid, sum(1 << e for e in es))
+        count["sent"] += len(es)
+        n = len(topo.engines(dst, core)[lo:hi])
+        count[sem] = n
+        note((sem, n, {sem: n}), [], out[1])
+
+    flip = [0]
+
+    def turn(pad, parts=(0, 1), into=None):
+        w = "tw%d" % flip[0] if into is None else into[1][0][0]
+        if into is None:
+            flip[0] = (flip[0] + 1) % 3
+        for i in parts:
+            o, a, n = ((0, 0, C + 32), (C + 32, 16, C))[i]
+            d, p = V(w, o, o + n), V(pad, a, a + n)
+            run("v", lambda: g.vector.transpose(d[0], p[0]), [d], [p])
+        return V(w)
+
+    def wrapped(out, w, k):
+        ts(out, pick(w, off(k)), 160.0, add)
+
+    def half(out, o, win, offs, a):
+        cp("v", V(out, o, o + HALF), pick(win, V(offs, a, a + 10)))
+        cp("s", V(out, o + HALF, o + C), pick(win, V(offs, a + 10, a + 20)))
+
+    def units(b):
+        e = (128 * b, 128 * b + 128)
+        quant(V("eq", *e), V("es", *e), V("et", 512 * b, 512 * b + 512))
+
+    c1 = lambda n: V(n, 0, 1)
+    c5 = lambda n: V(n, 0, 5)
+    L = lambda n, a=0, b=20: V(n, a, b)
+    off = lambda k: V("off", 0, k)
+    P16 = lambda n: V(n, 16, 16 + C)
+    row = lambda n, t, a=0, b=C: V(n, C * t + a, C * t + b)
+    partner = [T.cores[rank ^ m] for m in MASKS]
+
+    load("y", V("iP"), T.pb[:, :], "d_pb")
+    load("s", V("ut"), T.u[:, :], "d_u")
+    load("y", V("iE"), T.ex[:, :], "d_ex")
+    load("s", V("xi", 0, 4 * HALF), T.x[:, 0:4 * HALF], "d_x0")
+    load("y", V("iF"), T.fd[:, :], "d_fd")
+    load("s", V("xi", 4 * HALF, 4 * C), T.x[:, 4 * HALF:4 * C], "d_x1")
+    load("y", V("iY"), T.lg[:, :], "d_lg")
+
+    def iota(out, pattern, base, cm, small=False):
+        if small:
+            run("g", lambda: g.iota(out[0], pattern, base, cm, allow_small_or_imprecise_dtypes=True), [out], [])
+        else:
+            run("g", lambda: g.iota(out[0], pattern, base, cm), [out], [])
+
+    iota(V("ip"), [[0, 20]], 0, 1)
+    iota(V("ik"), [[16, 20]], 0, 0)
+    iota(V("idn"), [[1, C]], -HALF, 0, small=True)
+    run("v", lambda: g.vector.memset(T.ones[:, :], 1.0), [V("ones")], [])
+
+    def unit(b):
+        o, i = V("et", 512 * b, 512 * b + 512), V("ones")
+        run("g", lambda: g.affine_select(o[0], i[0], [[1, 512]], AluOpType.is_equal, 0.0, -b, -4), [o], [i])
+
+    send(partner[0], V("lp1"), V("iP"), "a_p1", 0, 4)
+    for b in range(4):
+        unit(b)
+    iota(V("idf"), [[1, C]], 0, 0, small=True)
+
+    cp("s", V("wf"), V("idn"))
+    for n in ("cb", "nm", "cc", "yb", "yf"):
+        for a in (0, 16 + C):
+            cp("s", V(n, a, a + 16), V("ones", 0, 16))
+    ts(V("i16"), V("ip"), 15, AluOpType.bitwise_and)
+    ts(c1("o1"), V("ip", 0, 1), 1, AluOpType.bitwise_and)
+    ts(c1("o2"), V("ip", 0, 1), 4, AluOpType.logical_shift_right, 1, AluOpType.bitwise_and)
+    tt(V("cw"), V("i16"), V("ik"), add)
+    tt(c1("f1"), c1("o1"), c1("o2"), AluOpType.is_equal)
+    ts(c5("o3"), V("cw", 0, 5), 3277, mul)
+    ts(c1("f2"), c1("f1"), 336.0, mul, 16.0, add)
+    ts(c5("o4"), c5("o3"), 16, AluOpType.arith_shift_right)
+    cp("v", V("bs", 0, 20), V("cw"))
+    cp("v", V("bs", 40, 60), V("cw"))
+    ts(c5("f3"), V("cw", 0, 5), 16.0, mul, c1("f2"), add)
+    ts(c5("f4"), c5("o4"), -319.0, mul)
+    tt(c5("f5"), c5("f3"), c5("f4"), add)
+    cp("v", c5("off"), c5("f5"))
+
+    cp("v", L("uP"), V("iP"))
+    cp("s", V("po"), pick(V("idn"), L("uP")))
+    cp("v", L("uE"), V("iE"))
+    cp("s", P16("cb"), pick(V("po"), L("uE")))
+    tt(V("iM"), V("iE"), V("cw"), AluOpType.min)
+    cp("v", L("uF"), V("iF"))
+    cp("s", V("fm"), pick(V("idn"), L("uF")))
+    cp("v", L("uM"), V("iM"))
+    cp("v", L("uY"), V("iY"))
+    order("y", V("fm")[1], V("wf")[1])
+    g.sync.dma_start(T.wf[1:128:16, :], T.fm[1:128:16, :]).then_inc(T.sem.d_wf, 16)
+    note(("d_wf", 16, {"d_wf": 16}), V("fm")[1], V("wf")[1])
+    load("y", V("wq"), T.wc[:, :], "d_wc", codes=True)
+    load("y", V("wp"), T.ws[:, :], "d_ws")
+    load("y", V("vt"), T.v[:, :], "d_v")
+    quant(V("uq"), V("us"), V("ut"))
+    halves = ((0, HALF, 0), (HALF, C, 512))
+    for a, b, o in halves:
+        quant(V("xq", a, b), V("xs", a, b), V("xi", 4 * a, 4 * b))
+        mm(V("psA", o, o + HALF), V("uq"), V("us"), V("xq", a, b), V("xs", a, b))
+    cp("v", V("bs", 20, 40), V("iP"))
+    cp("s", V("bs", 60, 80), V("bs", 20, 40))
+    tt(V("df", 0, 20), V("iE"), V("cw"), sub)
+    cp("s", V("df", 40, 60), V("df", 0, 20))
+
+    for r in (1, 2, 3):
+        R = str(r)
+        tu, yk, yg = "tu" + R, "yk" + R, "yg" + R
+        far = partner[r - 1]
+        if r == 1:
+            for a, b, o in halves:
+                ts(V("sg", a, b), V("psA", o, o + HALF), 0.0, less)
+            tc = turn("cb", (0,))
+            half("nm", 16, V("sg"), "uM", 0)
+            cp("s", V("ya"), pick(V("idn"), L("uY")))
+            cp("s", V("yc"), pick(V("ya"), L("uF")))
+            cp("s", V("ya"), pick(V("yc"), L("uF")))
+            turn("cb", (1,), tc)
+            tn = turn("nm")
+            wrapped(V("pe"), tc, 2)
+            ts(row("xg", 0), V("xi", 0, 4 * C, 4), 0.5, mul)
+            tt(V("df", 20, 40), L("pe"), V("bs", 20, 40), sub)
+            tt(V("df", 60, 80), L("pe"), V("bs", 20, 40), sub)
+        else:
+            if r == 2:
+                ts(V("sg", HALF, C), V("psA", 0, HALF), 0.0, less)
+            ty = turn("cc")
+            ts(V("sg", 0, HALF), V("psA", 512, 512 + HALF), 0.0, less)
+            half("nm", 16, V("sg"), "uM", 0)
+            for t in range(3):
+                cp("s", row("xg", t), V("xi", t, 4 * C, 4), scale=0.5)
+            wrapped(V("y3" + R), ty, 2)
+            tn = turn("nm")
+        pieces = ((32, 64), (0, 32), (64, 80))
+
+        def signed(i):
+            a, b = pieces[i]
+            tt(V("pr", a, b), pick(tn, V("off", a // 16, b // 16)), V("df", a, b), mul)
+
+        def based(i):
+            a, b = pieces[i]
+            tt(V("tb", a, b), V("pr", a, b), V("bs", a, b), add)
+
+        def listed(i):
+            a, b = pieces[i]
+            cp("v", V(tu, a, b), V("tb", a, b))
+
+        if r == 1:
+            pieces = ((0, 80),)
+            signed(0)
+            ts(row("xg", 1), V("xi", 1, 4 * C, 4), 0.5, mul)
+            based(0)
+            ts(row("xg", 2), V("xi", 2, 4 * C, 4), 0.5, mul)
+            listed(0)
+        else:
+            for call, i in ((signed, 0), (signed, 1), (based, 0), (signed, 2), (based, 1), (listed, 0), (based, 2), (listed, 1)):
+                call(i)
+
+        if r == 1:
+            cp("v", L("uR"), V("lp1"))
+            ts(row("xg", 3), V("xi", 3, 4 * C, 4), 0.5, mul)
+            half("pp", 0, V("wf"), "uR", 0)
+            cp("s", P16("cc"), pick(V("ya"), L("uF")))
+            cp("v", V("g1"), pick(V("pp"), V(tu, 40, 60)))
+            half("g2", 0, V("g1"), tu, 20)
+            ty = turn("cc", (0,))
+            half("g4", 0, V("g2"), "uR", 0)
+            turn("cc", (1,), ty)
+            half("g3", 0, V("g4"), tu, 0)
+            wrapped(V("y31"), ty, 2)
+        else:
+            half("g1", 0, V("pp"), tu, 40)
+            listed(2)
+            half("g2", 0, V("g1"), tu, 20)
+            ts(row("xg", 3), V("xi", 3, 4 * C, 4), 0.5, mul)
+            half("g3", 0, V("g2"), tu, 0)
+        if r < 3:
+            send(partner[r], V("lp%d" % (r + 1)), V(tu, 60, 80), "a_p%d" % (r + 1), 0, 8)
+        half("yb", 16, V("g3"), "y3" + R, 0)
+        if r == 1:
+            units(0)
+        cp("s", P16("yf"), pick(P16("yb"), L("uF")))
+        tn = turn("yb")
+        wrapped(V(yk, 0, 32), tn, 2)
+        if r == 1:
+            units(1)
+        else:
+            ts(V(yk, 32, 48), pick(tn, V("off", 2, 3)), 160.0, add)
+        lo, hi = (8, 16) if r == 1 else (0, 8)
+        kl = V("kl" + R, 0, 10)
+        send(far, kl, V(yk, 20, 30), "a_k" + R, lo, hi)
+
+        tf = turn("yf")
+        if r == 1:
+            ts(V(yk, 32, 48), pick(tn, V("off", 2, 3)), 160.0, add)
+        wrapped(V(yg), tf, 2)
+        for a, b in PIECES:
+            for t in range(4):
+                cp("s", row("ag", t, a, b), pick(row("xg", t), V(yk, a // 16, b // 16)))
+        for i, (a, b) in enumerate(PIECES):
+            ps = ("psA", "psB")[i]
+            for t in range(4):
+                tt(V("zt", 4 * a + t, 4 * b, 4), pick(row("xg", t), V(yg, a // 16, b // 16)), row("ag", t, a, b), add)
+            if r == 1 and i == 0:
+                units(3)
+            quant(V("zq", a, b), V("zs", a, b), V("zt", 4 * a, 4 * b))
+            for t in (0, 2, 1, 3):
+                w = (128 * t, 128 * t + 128)
+                mm(V(ps, 512 * t, 512 * t + b - a), V("wq", *w), V("wp", *w), V("zq", a, b), V("zs", a, b))
+
+        def made(q, i, t):
+            a, b = PIECES[i]
+            o, p = row("hg", t, a, b), V(("psA", "psB")[i], 512 * t, 512 * t + b - a)
+            if q == "v":
+                ts(o, p, 0.03125, mul)
+            else:
+                cp("s", o, p, scale=0.03125)
+
+        for q, t in (("s", 0), ("s", 2), ("s", 1), ("v", 3)):
+            made(q, 0, t)
+        if r == 1:
+            units(2)
+        made("v", 1, 0)
+        made("s", 1, 2)
+        made("s", 1, 1)
+        for q, c in (("v", 0), ("s", 2), ("v", 3), ("s", 1)):
+            if c == 3:
+                made("v", 1, 3)
+            cp(q, V("hf", c, 4 * HALF, 4), pick(row("hg", c), kl))
+        hq, hs, lq, lsc = (V(n + R) for n in ("hq", "hs", "lq", "ls"))
+        quant(hq, hs, V("hf"))
+        send(far, lq, hq, "a_q" + R, 0, 16, codes=True)
+        send(far, lsc, hs, "a_s" + R, 0, 16)
+
+        for t in range(4):
+            o = V("xi", 4 * HALF + t, 4 * C, 4)
+            tt(o, pick(row("hg", t), V(yk, 30, 40)), o, add)
+        xqo, xso = V("xq", HALF, C), V("xs", HALF, C)
+        quant(xqo, xso, V("xi", 4 * HALF, 4 * C))
+        if r < 3:
+            lp = V("lp%d" % (r + 1))
+            cp("s", L("t2"), V("pr", 60, 80), scale=-2.0)
+            cp("s", V("pp"), pick(V("wf"), lp))
+            cp("s", P16("cb"), pick(V("pp"), L("uE")))
+            cp("s", V("bs", 20, 40), V("tb", 60, 80))
+            cp("s", V("bs", 60, 80), V("tb", 60, 80))
+            tc = turn("cb")
+            cp("v", V("bs", 0, 20), lp)
+            tt(V("df", 20, 40), V("df", 60, 80), L("t2"), add)
+            wrapped(V("pe"), tc, 2)
+            if r == 2:
+                mm(V("psA", 0, HALF), V("uq"), V("us"), xqo, xso)
+                ts(V("sg", HALF, C), V("psA", 0, HALF), 0.0, less)
+            cp("s", V("ya"), pick(P16("yf"), L("uF")))
+            cp("s", P16("cc"), pick(V("ya"), L("uF")))
+            cp("s", V("df", 60, 80), V("df", 20, 40))
+        else:
+            quant(V("vq"), V("vs"), V("vt"))
+            store("y", T.oc[:, 4 * HALF:4 * C], xqo[0].bitcast(dt.uint8), xqo[1])
+            for k in range(4):
+                store("y", T.osc[4 * k:4 * k + 4, HALF:C], T.xs[32 * k:32 * k + 4, HALF:C], xso[1])
+            mm(V("psA", 0, HALF), V("vq"), V("vs"), xqo, xso)
+            cp("s", V("yo", HALF, C), V("psA", 0, HALF))
+            store("y", T.y[:, HALF:C], V("yo", HALF, C)[0], V("yo", HALF, C)[1])
+            cp("s", V("pout", 0, C), pick(V("idf"), L(yk)))
+            cp("s", V("pout", C, 2 * C), pick(V("idf"), V(tu, 60, 80)))
+            store("y", T.pl[:, :], T.pout[0:128:16, :], V("pout")[1])
+
+        for t in range(4):
+            e = (128 * t, 128 * t + 128)
+            mm(V("psB", 512 * t, 512 * t + HALF), V("eq", *e), V("es", *e), lq, lsc)
+        if r == 1:
+            mm(V("psA", 0, HALF), V("uq"), V("us"), xqo, xso)
+        for t in range(4):
+            o = V("xi", t, 4 * HALF, 4)
+            tt(o, V("psB", 512 * t, 512 * t + HALF), o, add)
+        if r < 3:
+            tt(V("df", 0, 20), L("pe"), V("bs", 0, 20), sub)
+        xqf, xsf = V("xq", 0, HALF), V("xs", 0, HALF)
+        quant(xqf, xsf, V("xi", 0, 4 * HALF))
+        if r < 3:
+            mm(V("psA", 512, 512 + HALF), V("uq"), V("us"), xqf, xsf)
+        else:
+            mm(V("psA", 512, 512 + HALF), V("vq"), V("vs"), xqf, xsf)
+            store("y", T.oc[:, 0:4 * HALF], xqf[0].bitcast(dt.uint8), xqf[1])
+            for k in range(4):
+                store("ys"[k % 2], T.osc[4 * k:4 * k + 4, 0:HALF], T.xs[32 * k:32 * k + 4, 0:HALF], xsf[1])
+            cp("v", V("yo", 0, HALF), V("psA", 512, 512 + HALF))
+            store("s", T.y[:, 0:HALF], V("yo", 0, HALF)[0], V("yo", 0, HALF)[1])
+
+    for s in ["c_v", "c_s", "c_t", "c_g"] + ARRIVALS + ["sent", "stored"]:
+        g.wait_ge(T.sem[s], count[s])
+    for s in LOADS:
+        g.wait_ge(T.sem[s], 16)

@@ -2,53 +2,70 @@ from concourse.mybir import dt, AluOpType, ActivationFunctionType
 
 C, HALF = 320, 160
 MASKS = (1, 2, 4)
-PIECES = ((0, 192), (192, 320))
+CUT = 192
+RUN = {"a": (0, CUT), "b": (CUT, C), "f": (0, HALF), "n": (HALF, C), "w": (0, C)}
+
+LOADORDER = "y:pb s:lg y:fd s:ex y:u s:x0 y:x1"
+FIRST = ("uFY uE uP sendP po ya yc:0 wd qf pE uq iM mf qn later uM d0 e0 off sfv mn snv bP X0wv nm cb0 cb1 yd cc nm1 nm0 d1 p2 p0 b2 p3 "
+         "b0 l2 pq:128 l0 cc1 cc0 g1 y3 g2 ofa ofb g4 b3 g3 l3 sendB X1wv yb X2wv ")
+SIGNS = "cc0 cc1 sfv nm y3 nm0 nm1 c2 p1 pz k2 b1 bz g1:96 l1 lz g2 p3 g3 b3 yb l3 sendB "
+LAYER = ("F0s F1s yb0a yb1a yb0b yb1b wYa yf0a yf1a wYb yf0b yf1b wGa wKa sendK wGb A0a A1a A2a A3a A0b A1b A2b A3b "
+         "Z0a Z1a Z2a Z3a Z0b qa Z1b Z2b Z3b wKb qb "
+         "H0as H2as H1as H3av H0bv H2bv H1bs f0v f2s H3bv f3v f1s hq ")
+FLIGHT = "n0 n1 n2 n3 qn pq:0 cb t2 cc X0ns X1ns X2ns X3ns mn sns bF cb0 cb1 dP un a0 a1 a2 a3 dF qf X0fs X1fs X2fs X3fs mf "
+LAST = "n0 n1 n2 n3 qn vq on mn pl yn un a0 a1 a2 a3 qf mf of yo"
+ROUNDS = (FIRST + LAYER.replace("A0a", "X3wv A0a").replace("qb", "e1 qb").replace("H3av", "H3av e2").replace("hq", "e3 hq") + FLIGHT,
+          SIGNS + LAYER + FLIGHT, SIGNS.replace("sendB ", "") + LAYER + LAST)
 
 SCRATCH = {
     "xi": ("sbuf", [128, 4 * C], "bfloat16"), "xg": ("sbuf", [128, 4 * C], "bfloat16"),
     "ag": ("sbuf", [128, 4 * C], "bfloat16"), "zt": ("sbuf", [128, 4 * C], "bfloat16"),
     "hg": ("sbuf", [128, 4 * C], "bfloat16"), "hf": ("sbuf", [128, 4 * HALF], "bfloat16"),
     "ut": ("sbuf", [128, 512], "bfloat16"), "vt": ("sbuf", [128, 512], "bfloat16"),
-    "ones": ("sbuf", [128, 512], "bfloat16"), "et": ("sbuf", [128, 2048], "bfloat16"),
+    "ones": ("sbuf", [128, 516], "bfloat16"), "et": ("sbuf", [128, 516], "bfloat16"),
     "uq": ("sbuf", [128, 128], "float8_e4m3fn_x4"), "us": ("sbuf", [128, 128], "uint8"),
     "vq": ("sbuf", [128, 128], "float8_e4m3fn_x4"), "vs": ("sbuf", [128, 128], "uint8"),
     "wq": ("sbuf", [128, 512], "float8_e4m3fn_x4"), "wp": ("sbuf", [128, 512], "uint8"),
     "eq": ("sbuf", [128, 512], "float8_e4m3fn_x4"), "es": ("sbuf", [128, 512], "uint8"),
     "xq": ("sbuf", [128, C], "float8_e4m3fn_x4"), "xs": ("sbuf", [128, C], "uint8"),
-    "zq": ("sbuf", [128, C], "float8_e4m3fn_x4"), "zs": ("sbuf", [128, C], "uint8"),
-    "iY": ("sbuf", [128, 20], "int32"), "iP": ("sbuf", [128, 20], "int32"),
-    "iF": ("sbuf", [128, 20], "int32"), "iE": ("sbuf", [128, 20], "int32"),
-    "uY": ("sbuf", [128, 32], "uint16"), "uP": ("sbuf", [128, 32], "uint16"),
-    "uF": ("sbuf", [128, 32], "uint16"), "uE": ("sbuf", [128, 32], "uint16"),
-    "uM": ("sbuf", [128, 32], "uint16"), "uR": ("sbuf", [128, 32], "uint16"),
-    "off": ("sbuf", [128, 16], "uint16"),
-    "ip": ("sbuf", [128, 20], "int32"), "ik": ("sbuf", [128, 20], "int32"),
-    "i16": ("sbuf", [128, 20], "int32"), "cw": ("sbuf", [128, 20], "int32"), "iM": ("sbuf", [128, 20], "int32"),
-    "o1": ("sbuf", [128, 8], "int32"), "o2": ("sbuf", [128, 8], "int32"), "o3": ("sbuf", [128, 8], "int32"),
-    "o4": ("sbuf", [128, 8], "int32"),
-    "f1": ("sbuf", [128, 8], "float32"), "f2": ("sbuf", [128, 8], "float32"), "f3": ("sbuf", [128, 8], "float32"),
-    "f4": ("sbuf", [128, 8], "float32"), "f5": ("sbuf", [128, 8], "float32"),
-    "bs": ("sbuf", [128, 80], "float32"), "df": ("sbuf", [128, 80], "float32"),
-    "pr": ("sbuf", [128, 80], "float32"), "tb": ("sbuf", [128, 80], "float32"),
-    "pe": ("sbuf", [128, 32], "float32"), "t2": ("sbuf", [128, 32], "float32"),
-    "idn": ("sbuf", [128, C], "bfloat16"), "fm": ("sbuf", [128, C], "bfloat16"),
+    "zqa": ("sbuf", [128, C], "float8_e4m3fn_x4"), "zsa": ("sbuf", [128, C], "uint8"),
+    "zqb": ("sbuf", [128, C], "float8_e4m3fn_x4"), "zsb": ("sbuf", [128, C], "uint8"),
+    "iP": ("sbuf", [128, 32], "int32"), "iE": ("sbuf", [128, 32], "int32"), "iFY": ("sbuf", [128, 40], "int32"),
+    "uP": ("sbuf", [128, 32], "uint16"), "uE": ("sbuf", [128, 32], "uint16"), "uFY": ("sbuf", [128, 48], "uint16"),
+    "uM": ("sbuf", [128, 32], "uint16"), "off": ("sbuf", [128, 16], "uint16"),
+    "i17": ("sbuf", [128, 8], "int32"), "ik": ("sbuf", [128, 32], "int32"), "i8": ("sbuf", [128, 8], "int32"),
+    "i16": ("sbuf", [128, 8], "int32"), "par": ("sbuf", [128, 8], "int32"), "iM": ("sbuf", [128, 32], "float32"),
+    "f1": ("sbuf", [128, 8], "float32"), "f2": ("sbuf", [128, 8], "float32"), "f16": ("sbuf", [128, 8], "float32"),
+    "m0": ("sbuf", [128, 8], "float32"), "m1": ("sbuf", [128, 8], "float32"),
+    "pr": ("sbuf", [128, 128], "float32"), "tb": ("sbuf", [128, 96], "float32"),
+    "cw": ("sbuf", [128, 32], "float32"), "t2": ("sbuf", [128, 32], "float32"),
+    "idn": ("sbuf", [128, C], "bfloat16"), "idk": ("sbuf", [128, C], "bfloat16"), "id0": ("sbuf", [128, C], "bfloat16"),
     "wf": ("sbuf", [128, C], "bfloat16"), "pp": ("sbuf", [128, C], "bfloat16"), "po": ("sbuf", [128, C], "bfloat16"),
     "sg": ("sbuf", [128, C], "bfloat16"), "g1": ("sbuf", [128, C], "bfloat16"), "g2": ("sbuf", [128, C], "bfloat16"),
     "g3": ("sbuf", [128, C], "bfloat16"), "g4": ("sbuf", [128, C], "bfloat16"), "ya": ("sbuf", [128, C], "bfloat16"),
-    "yc": ("sbuf", [128, C], "bfloat16"), "yf": ("sbuf", [128, C + 32], "bfloat16"),
-    "nm": ("sbuf", [128, C + 32], "bfloat16"), "yb": ("sbuf", [128, C + 32], "bfloat16"),
-    "cb": ("sbuf", [128, C + 32], "bfloat16"), "cc": ("sbuf", [128, C + 32], "bfloat16"),
-    "idf": ("sbuf", [128, C], "float32"),
-    "tw2": ("sbuf", [128, 2 * C + 32], "bfloat16"), "tw0": ("sbuf", [128, 2 * C + 32], "bfloat16"), "tw1": ("sbuf", [128, 2 * C + 32], "bfloat16"),
+    "yc": ("sbuf", [128, C], "bfloat16"), "yd": ("sbuf", [128, C], "bfloat16"),
+    "tnm": ("sbuf", [128, 2 * C + 32], "bfloat16"), "tyb": ("sbuf", [128, 2 * C + 64], "bfloat16"),
+    "tyf": ("sbuf", [128, 2 * C + 64], "bfloat16"), "tcb": ("sbuf", [128, 2 * C + 32], "bfloat16"),
+    "tcc": ("sbuf", [128, 2 * C + 32], "bfloat16"),
     "yo": ("sbuf", [128, C], "float32"), "pout": ("sbuf", [128, 2 * C], "float32"),
-    "lp1": ("sbuf", [128, 20], "int32"), "lp2": ("sbuf", [128, 20], "uint16"), "lp3": ("sbuf", [128, 20], "uint16"),
     "psA": ("psum", [128, 2048], "float32"), "psB": ("psum", [128, 2048], "float32"),
+    "bs4": ("sbuf", [128, 64], "float32"),
 }
+PADDED = ("cb", "nm", "cc", "yb", "yf")
+for _n in PADDED:
+    SCRATCH[_n] = ("sbuf", [128, C + 32], "bfloat16")
+SCRATCH["cb"] = ("sbuf", [128, 2 * C + 32], "bfloat16")
+for _n in ("fa", "fb", "m2", "mv", "ms"):
+    SCRATCH[_n] = ("sbuf", [128, 8], "float32")
+TURNS = {"0": (0, 0, C + 32), "1": (C + 32, 16, C), "0a": (0, 0, 224), "1a": (224, 16, 192), "0b": (416, 192, 160), "1b": (576, 208, 128)}
 for _r in "123":
-    SCRATCH["tu" + _r] = ("sbuf", [128, 80], "uint16")
-    SCRATCH["yk" + _r] = ("sbuf", [128, 48], "uint16")
+    SCRATCH["lp" + _r] = ("sbuf", [128, 32], "uint16")
+    SCRATCH["bs" + _r] = ("sbuf", [128, 64], "float32")
+    SCRATCH["df" + _r] = ("sbuf", [128, 64], "float32")
+    SCRATCH["tu" + _r] = ("sbuf", [128, 128], "uint16")
+    SCRATCH["yk" + _r] = ("sbuf", [128, 64], "uint16")
     SCRATCH["yg" + _r] = ("sbuf", [128, 32], "uint16")
-    SCRATCH["y3" + _r] = ("sbuf", [128, 32], "uint16")
+    SCRATCH["y3" + _r] = ("sbuf", [128, 64], "uint16")
     SCRATCH["kl" + _r] = ("sbuf", [128, 16], "uint16")
     SCRATCH["hq" + _r] = ("sbuf", [128, HALF], "float8_e4m3fn_x4")
     SCRATCH["hs" + _r] = ("sbuf", [128, HALF], "uint8")
@@ -68,7 +85,7 @@ def rank_program(g, core, T, topo):
     count = {"c_v": 0, "c_s": 0, "c_t": 0, "c_g": 0, "sent": 0, "stored": 0}
     known = {q: {} for q in queue}
     touched = {n: [] for n in SCRATCH}
-    copy = ActivationFunctionType.Copy
+    copy, ident = ActivationFunctionType.Copy, ActivationFunctionType.Identity
     add, sub, mul, less = AluOpType.add, AluOpType.subtract, AluOpType.mult, AluOpType.is_lt
 
     def meets(a, b):
@@ -125,11 +142,17 @@ def rank_program(g, core, T, topo):
     def pick(win, off):
         return (win[0].indirect(off[0]), win[1] + off[1])
 
-    def cp(q, out, in_, scale=None):
-        if q == "v":
+    def cp(q, out, in_, scale=None, bias=None):
+        if q == "v" and scale is not None:
+            ts(out, in_, scale, mul)
+        elif q == "v":
             run(q, lambda: g.vector.tensor_copy(out[0], in_[0]), [out], [in_])
+        elif isinstance(scale, tuple):
+            run(q, lambda: g.scalar.activation(out[0], in_[0], copy, scale=scale[0]), [out], [in_, scale])
         elif scale is not None:
             run(q, lambda: g.scalar.activation(out[0], in_[0], copy, scale=scale), [out], [in_])
+        elif bias is not None:
+            run(q, lambda: g.scalar.activation(out[0], in_[0], ident, bias=bias), [out], [in_])
         else:
             run(q, lambda: g.scalar.activation(out[0], in_[0], copy), [out], [in_])
 
@@ -144,6 +167,9 @@ def rank_program(g, core, T, topo):
             run("v", lambda: g.vector.tensor_scalar(out[0], a[0], p1, None, op0), [out], [a] + cols)
         else:
             run("v", lambda: g.vector.tensor_scalar(out[0], a[0], p1, p2, op0, op1), [out], [a] + cols)
+
+    def fill(out, value):
+        run("v", lambda: g.vector.memset(out[0], value), [out], [])
 
     def quant(q, s, t):
         run("v", lambda: g.vector.quantize_mx(q[0], s[0], t[0]), [q, s], [t])
@@ -173,295 +199,257 @@ def rank_program(g, core, T, topo):
         count[sem] = n
         note((sem, n, {sem: n}), [], out[1])
 
-    flip = [0]
+    def turn(n, i):
+        o, a, k = TURNS[i]
+        a += C if n == "cb" else 0
+        d, p = V("t" + n, o, o + k), V(n, a, a + k)
+        run("v", lambda: g.vector.transpose(d[0], p[0]), [d], [p])
 
-    def turn(pad, parts=(0, 1), into=None):
-        w = "tw%d" % flip[0] if into is None else into[1][0][0]
-        if into is None:
-            flip[0] = (flip[0] + 1) % 3
-        for i in parts:
-            o, a, n = ((0, 0, C + 32), (C + 32, 16, C))[i]
-            d, p = V(w, o, o + n), V(pad, a, a + n)
-            run("v", lambda: g.vector.transpose(d[0], p[0]), [d], [p])
-        return V(w)
+    def part(out, o, n, j, h):
+        w, a = (V("t" + n, 0, 416), 0) if h == "a" else (V("t" + n, 416, 704), CUT // 16 if j else 16)
+        f = 8 + 2 * j + (0 if h == "a" else 4)
+        ts(V(out, o + a, o + a + 16), pick(w, V("off", f, f + 1)), float(HALF), add)
 
-    def wrapped(out, w, k):
-        ts(out, pick(w, off(k)), 160.0, add)
+    def wrapped(out, n, j, k=1):
+        ts(out, pick(V("t" + n, 0, 2 * C + 32), off(j, k)), float(HALF), add)
 
-    def half(out, o, win, offs, a):
-        cp("v", V(out, o, o + HALF), pick(win, V(offs, a, a + 10)))
-        cp("s", V(out, o + HALF, o + C), pick(win, V(offs, a + 10, a + 20)))
-
-    def units(b):
-        e = (128 * b, 128 * b + 128)
-        quant(V("eq", *e), V("es", *e), V("et", 512 * b, 512 * b + 512))
+    def shared(out, o, win, offs, a, cut):
+        if cut > 0:
+            cp("v", V(out, o, o + cut), pick(win, V(offs, a, a + cut // 16)))
+        if cut < C:
+            cp("s", V(out, o + cut, o + C), pick(win, V(offs, a + cut // 16, a + 20)))
 
     c1 = lambda n: V(n, 0, 1)
-    c5 = lambda n: V(n, 0, 5)
-    L = lambda n, a=0, b=20: V(n, a, b)
-    off = lambda k: V("off", 0, k)
-    P16 = lambda n: V(n, 16, 16 + C)
+    L = lambda n, a=0: V(n, a, a + 20)
+    W = lambda n, j, k=1: V(n, 32 * j, 32 * (j + k))
+    off = lambda j, k=1: V("off", 2 * j, 2 * (j + k))
+    P16 = lambda n: V(n, C + 16, 2 * C + 16) if n == "cb" else V(n, 16, 16 + C)
     row = lambda n, t, a=0, b=C: V(n, C * t + a, C * t + b)
+    mixed = lambda n, t, a, b: V(n, 4 * a + t, 4 * b, 4)
     partner = [T.cores[rank ^ m] for m in MASKS]
+    uF, uY = L("uFY"), L("uFY", 20)
 
-    load("y", V("iP"), T.pb[:, :], "d_pb")
-    load("s", V("ut"), T.u[:, :], "d_u")
-    load("y", V("iE"), T.ex[:, :], "d_ex")
-    load("s", V("xi", 0, 4 * HALF), T.x[:, 0:4 * HALF], "d_x0")
-    load("y", V("iF"), T.fd[:, :], "d_fd")
-    load("s", V("xi", 4 * HALF, 4 * C), T.x[:, 4 * HALF:4 * C], "d_x1")
-    load("y", V("iY"), T.lg[:, :], "d_lg")
+    first = {"pb": (L("iP"), T.pb[:, :]), "u": (V("ut"), T.u[:, :]), "ex": (L("iE"), T.ex[:, :]), "lg": (L("iFY", 20), T.lg[:, :]),
+             "fd": (L("iFY"), T.fd[:, :]), "x0": (V("xi", 0, 4 * HALF), T.x[:, 0:4 * HALF]),
+             "x1": (V("xi", 4 * HALF, 4 * C), T.x[:, 4 * HALF:4 * C])}
+    for s in LOADORDER.split():
+        q, n = s.split(":")
+        load(q, first[n][0], first[n][1], "d_" + n)
 
-    def iota(out, pattern, base, cm, small=False):
-        if small:
-            run("g", lambda: g.iota(out[0], pattern, base, cm, allow_small_or_imprecise_dtypes=True), [out], [])
-        else:
-            run("g", lambda: g.iota(out[0], pattern, base, cm), [out], [])
+    def later():
+        order("y", V("xi")[1], [])
+        load("y", V("wq"), T.wc[:, :], "d_wc", codes=True)
+        load("y", V("wp"), T.ws[:, :], "d_ws")
+        load("y", V("vt"), T.v[:, :], "d_v")
 
-    iota(V("ip"), [[0, 20]], 0, 1)
-    iota(V("ik"), [[16, 20]], 0, 0)
-    iota(V("idn"), [[1, C]], -HALF, 0, small=True)
-    run("v", lambda: g.vector.memset(T.ones[:, :], 1.0), [V("ones")], [])
+    def moved():
+        order("y", V("yc")[1], V("id0")[1])
+        g.sync.dma_start(T.id0[1:128:16, :], T.yc[1:128:16, :]).then_inc(T.sem.d_wf, 16)
+        note(("d_wf", 16, {"d_wf": 16}), V("yc")[1], V("id0")[1])
 
-    def unit(b):
-        o, i = V("et", 512 * b, 512 * b + 512), V("ones")
-        run("g", lambda: g.affine_select(o[0], i[0], [[1, 512]], AluOpType.is_equal, 0.0, -b, -4), [o], [i])
+    def iota(out, pattern, base, cm):
+        run("g", lambda: g.iota(out[0], pattern, base, cm), [out], [])
 
-    send(partner[0], V("lp1"), V("iP"), "a_p1", 0, 4)
-    for b in range(4):
-        unit(b)
-    iota(V("idf"), [[1, C]], 0, 0, small=True)
+    iota(c1("i17"), [[0, 1]], 0, 17)
+    iota(V("ik"), [[16, 32]], 0, 0)
+    fill(V("ones"), 1.0)
+    o, i = V("et"), V("ones")
+    run("g", lambda: g.affine_select(o[0], i[0], [[1, 516]], AluOpType.is_equal, 0.0, -3, -4), [o], [i])
+    iota(V("i8"), [[1, 4], [256, 2]], 0, 0)
 
-    cp("s", V("wf"), V("idn"))
-    for n in ("cb", "nm", "cc", "yb", "yf"):
-        for a in (0, 16 + C):
+    ts(c1("i16"), c1("i17"), 15, AluOpType.bitwise_and)
+    ts(c1("par"), c1("i17"), 4, AluOpType.logical_shift_right, 1, AluOpType.bitwise_and)
+    d, one = V("idn"), V("ones", 0, C)
+    run("v", lambda: g.vector.tensor_tensor_scan(d[0], one[0], one[0], -HALF - 1.0, mul, add), [d], [one])
+    ts(c1("m0"), c1("i16"), 1.0, AluOpType.not_equal)
+    ts(c1("m1"), c1("i16"), 1.0, AluOpType.is_equal)
+    ts(c1("f1"), c1("par"), -336.0, mul, 352.0, add)
+    cp("v", c1("f16"), c1("i16"))
+    fill(V("iP", 20, 32), 0)
+    ts(c1("f2"), c1("i16"), 16.0, mul, c1("f1"), add)
+    ts(V("cw"), V("ik"), c1("f16"), add)
+    ts(W("bs1", 0), V("ik"), c1("f16"), add, -float(HALF), add)
+    fill(V("iE", 20, 32), 0)
+    ts(c1("fa"), c1("par"), 128.0, mul, -128.0, add)
+    ts(c1("fb"), c1("par"), 192.0, mul, -192.0, add)
+    ts(c1("m2"), c1("i16"), 2.0, AluOpType.is_equal, C + 15.0, mul)
+    tt(c1("fa"), c1("fa"), c1("f2"), add)
+    tt(c1("fb"), c1("fb"), c1("f2"), add)
+    ts(c1("mv"), c1("m2"), 1.0, add)
+    ts(c1("ms"), c1("m2"), 1.0, add, -1.0, mul)
+    cp("s", V("id0"), V("idn"), scale=c1("m0"))
+    cp("s", V("idk"), V("idn"), scale=c1("m1"))
+    for n in PADDED:
+        for a in (C, 2 * C + 16) if n == "cb" else (0, 16 + C):
             cp("s", V(n, a, a + 16), V("ones", 0, 16))
-    ts(V("i16"), V("ip"), 15, AluOpType.bitwise_and)
-    ts(c1("o1"), V("ip", 0, 1), 1, AluOpType.bitwise_and)
-    ts(c1("o2"), V("ip", 0, 1), 4, AluOpType.logical_shift_right, 1, AluOpType.bitwise_and)
-    tt(V("cw"), V("i16"), V("ik"), add)
-    tt(c1("f1"), c1("o1"), c1("o2"), AluOpType.is_equal)
-    ts(c5("o3"), V("cw", 0, 5), 3277, mul)
-    ts(c1("f2"), c1("f1"), 336.0, mul, 16.0, add)
-    ts(c5("o4"), c5("o3"), 16, AluOpType.arith_shift_right)
-    cp("v", V("bs", 0, 20), V("cw"))
-    cp("v", V("bs", 40, 60), V("cw"))
-    ts(c5("f3"), V("cw", 0, 5), 16.0, mul, c1("f2"), add)
-    ts(c5("f4"), c5("o4"), -319.0, mul)
-    tt(c5("f5"), c5("f3"), c5("f4"), add)
-    cp("v", c5("off"), c5("f5"))
 
-    cp("v", L("uP"), V("iP"))
-    cp("s", V("po"), pick(V("idn"), L("uP")))
-    cp("v", L("uE"), V("iE"))
-    cp("s", P16("cb"), pick(V("po"), L("uE")))
-    tt(V("iM"), V("iE"), V("cw"), AluOpType.min)
-    cp("v", L("uF"), V("iF"))
-    cp("s", V("fm"), pick(V("idn"), L("uF")))
-    cp("v", L("uM"), V("iM"))
-    cp("v", L("uY"), V("iY"))
-    order("y", V("fm")[1], V("wf")[1])
-    g.sync.dma_start(T.wf[1:128:16, :], T.fm[1:128:16, :]).then_inc(T.sem.d_wf, 16)
-    note(("d_wf", 16, {"d_wf": 16}), V("fm")[1], V("wf")[1])
-    load("y", V("wq"), T.wc[:, :], "d_wc", codes=True)
-    load("y", V("wp"), T.ws[:, :], "d_ws")
-    load("y", V("vt"), T.v[:, :], "d_v")
-    quant(V("uq"), V("us"), V("ut"))
-    halves = ((0, HALF, 0), (HALF, C, 512))
-    for a, b, o in halves:
-        quant(V("xq", a, b), V("xs", a, b), V("xi", 4 * a, 4 * b))
-        mm(V("psA", o, o + HALF), V("uq"), V("us"), V("xq", a, b), V("xs", a, b))
-    cp("v", V("bs", 20, 40), V("iP"))
-    cp("s", V("bs", 60, 80), V("bs", 20, 40))
-    tt(V("df", 0, 20), V("iE"), V("cw"), sub)
-    cp("s", V("df", 40, 60), V("df", 0, 20))
-
-    for r in (1, 2, 3):
-        R = str(r)
-        tu, yk, yg = "tu" + R, "yk" + R, "yg" + R
-        far = partner[r - 1]
-        if r == 1:
-            for a, b, o in halves:
-                ts(V("sg", a, b), V("psA", o, o + HALF), 0.0, less)
-            tc = turn("cb", (0,))
-            half("nm", 16, V("sg"), "uM", 0)
-            cp("s", V("ya"), pick(V("idn"), L("uY")))
-            cp("s", V("yc"), pick(V("ya"), L("uF")))
-            cp("s", V("ya"), pick(V("yc"), L("uF")))
-            turn("cb", (1,), tc)
-            tn = turn("nm")
-            wrapped(V("pe"), tc, 2)
-            ts(row("xg", 0), V("xi", 0, 4 * C, 4), 0.5, mul)
-            tt(V("df", 20, 40), L("pe"), V("bs", 20, 40), sub)
-            tt(V("df", 60, 80), L("pe"), V("bs", 20, 40), sub)
-        else:
-            if r == 2:
-                ts(V("sg", HALF, C), V("psA", 0, HALF), 0.0, less)
-            ty = turn("cc")
-            ts(V("sg", 0, HALF), V("psA", 512, 512 + HALF), 0.0, less)
-            half("nm", 16, V("sg"), "uM", 0)
-            for t in range(3):
-                cp("s", row("xg", t), V("xi", t, 4 * C, 4), scale=0.5)
-            wrapped(V("y3" + R), ty, 2)
-            tn = turn("nm")
-        pieces = ((32, 64), (0, 32), (64, 80))
-
-        def signed(i):
-            a, b = pieces[i]
-            tt(V("pr", a, b), pick(tn, V("off", a // 16, b // 16)), V("df", a, b), mul)
-
-        def based(i):
-            a, b = pieces[i]
-            tt(V("tb", a, b), V("pr", a, b), V("bs", a, b), add)
-
-        def listed(i):
-            a, b = pieces[i]
-            cp("v", V(tu, a, b), V("tb", a, b))
-
-        if r == 1:
-            pieces = ((0, 80),)
-            signed(0)
-            ts(row("xg", 1), V("xi", 1, 4 * C, 4), 0.5, mul)
-            based(0)
-            ts(row("xg", 2), V("xi", 2, 4 * C, 4), 0.5, mul)
-            listed(0)
-        else:
-            for call, i in ((signed, 0), (signed, 1), (based, 0), (signed, 2), (based, 1), (listed, 0), (based, 2), (listed, 1)):
-                call(i)
-
-        if r == 1:
-            cp("v", L("uR"), V("lp1"))
-            ts(row("xg", 3), V("xi", 3, 4 * C, 4), 0.5, mul)
-            half("pp", 0, V("wf"), "uR", 0)
-            cp("s", P16("cc"), pick(V("ya"), L("uF")))
-            cp("v", V("g1"), pick(V("pp"), V(tu, 40, 60)))
-            half("g2", 0, V("g1"), tu, 20)
-            ty = turn("cc", (0,))
-            half("g4", 0, V("g2"), "uR", 0)
-            turn("cc", (1,), ty)
-            half("g3", 0, V("g4"), tu, 0)
-            wrapped(V("y31"), ty, 2)
-        else:
-            half("g1", 0, V("pp"), tu, 40)
-            listed(2)
-            half("g2", 0, V("g1"), tu, 20)
-            ts(row("xg", 3), V("xi", 3, 4 * C, 4), 0.5, mul)
-            half("g3", 0, V("g2"), tu, 0)
-        if r < 3:
-            send(partner[r], V("lp%d" % (r + 1)), V(tu, 60, 80), "a_p%d" % (r + 1), 0, 8)
-        half("yb", 16, V("g3"), "y3" + R, 0)
-        if r == 1:
-            units(0)
-        cp("s", P16("yf"), pick(P16("yb"), L("uF")))
-        tn = turn("yb")
-        wrapped(V(yk, 0, 32), tn, 2)
-        if r == 1:
-            units(1)
-        else:
-            ts(V(yk, 32, 48), pick(tn, V("off", 2, 3)), 160.0, add)
-        lo, hi = (8, 16) if r == 1 else (0, 8)
-        kl = V("kl" + R, 0, 10)
-        send(far, kl, V(yk, 20, 30), "a_k" + R, lo, hi)
-
-        tf = turn("yf")
-        if r == 1:
-            ts(V(yk, 32, 48), pick(tn, V("off", 2, 3)), 160.0, add)
-        wrapped(V(yg), tf, 2)
-        for a, b in PIECES:
-            for t in range(4):
-                cp("s", row("ag", t, a, b), pick(row("xg", t), V(yk, a // 16, b // 16)))
-        for i, (a, b) in enumerate(PIECES):
-            ps = ("psA", "psB")[i]
-            for t in range(4):
-                tt(V("zt", 4 * a + t, 4 * b, 4), pick(row("xg", t), V(yg, a // 16, b // 16)), row("ag", t, a, b), add)
-            if r == 1 and i == 0:
-                units(3)
-            quant(V("zq", a, b), V("zs", a, b), V("zt", 4 * a, 4 * b))
-            for t in (0, 2, 1, 3):
-                w = (128 * t, 128 * t + 128)
-                mm(V(ps, 512 * t, 512 * t + b - a), V("wq", *w), V("wp", *w), V("zq", a, b), V("zs", a, b))
-
-        def made(q, i, t):
-            a, b = PIECES[i]
-            o, p = row("hg", t, a, b), V(("psA", "psB")[i], 512 * t, 512 * t + b - a)
-            if q == "v":
-                ts(o, p, 0.03125, mul)
-            else:
-                cp("s", o, p, scale=0.03125)
-
-        for q, t in (("s", 0), ("s", 2), ("s", 1), ("v", 3)):
-            made(q, 0, t)
-        if r == 1:
-            units(2)
-        made("v", 1, 0)
-        made("s", 1, 2)
-        made("s", 1, 1)
-        for q, c in (("v", 0), ("s", 2), ("v", 3), ("s", 1)):
-            if c == 3:
-                made("v", 1, 3)
-            cp(q, V("hf", c, 4 * HALF, 4), pick(row("hg", c), kl))
+    def calls(r):
+        R, N = str(r), str(r + 1)
+        tu, yk, yg, bs, df, nbs, ndf, lp = "tu" + R, "yk" + R, "yg" + R, "bs" + R, "df" + R, "bs" + N, "df" + N, "lp" + N
+        far, kl = partner[r - 1], V("kl" + R, 0, 10)
         hq, hs, lq, lsc = (V(n + R) for n in ("hq", "hs", "lq", "ls"))
-        quant(hq, hs, V("hf"))
-        send(far, lq, hq, "a_q" + R, 0, 16, codes=True)
-        send(far, lsc, hs, "a_s" + R, 0, 16)
+        bank = {"n": 0, "f": 512}
+        xq = lambda h: (V("xq", *RUN[h]), V("xs", *RUN[h]))
+        score = lambda h: V("psA", bank[h], bank[h] + HALF)
 
-        for t in range(4):
-            o = V("xi", 4 * HALF + t, 4 * C, 4)
-            tt(o, pick(row("hg", t), V(yk, 30, 40)), o, add)
-        xqo, xso = V("xq", HALF, C), V("xs", HALF, C)
-        quant(xqo, xso, V("xi", 4 * HALF, 4 * C))
-        if r < 3:
-            lp = V("lp%d" % (r + 1))
-            cp("s", L("t2"), V("pr", 60, 80), scale=-2.0)
-            cp("s", V("pp"), pick(V("wf"), lp))
-            cp("s", P16("cb"), pick(V("pp"), L("uE")))
-            cp("s", V("bs", 20, 40), V("tb", 60, 80))
-            cp("s", V("bs", 60, 80), V("tb", 60, 80))
-            tc = turn("cb")
-            cp("v", V("bs", 0, 20), lp)
-            tt(V("df", 20, 40), V("df", 60, 80), L("t2"), add)
-            wrapped(V("pe"), tc, 2)
-            if r == 2:
-                mm(V("psA", 0, HALF), V("uq"), V("us"), xqo, xso)
-                ts(V("sg", HALF, C), V("psA", 0, HALF), 0.0, less)
-            cp("s", V("ya"), pick(P16("yf"), L("uF")))
-            cp("s", P16("cc"), pick(V("ya"), L("uF")))
-            cp("s", V("df", 60, 80), V("df", 20, 40))
-        else:
-            quant(V("vq"), V("vs"), V("vt"))
-            store("y", T.oc[:, 4 * HALF:4 * C], xqo[0].bitcast(dt.uint8), xqo[1])
+        def made(h, t, a):
+            o = 512 * t - min(RUN[h][0], C - 128)
+            return V("psA" if h == "a" else "psB", o + a, o + RUN[h][1])
+
+        seen = {}
+
+        def again(n):
+            seen[n] = seen.get(n, 0) + 1
+            return r > 1 or seen[n] > 1
+
+        def layer(h):
+            a, b = min(RUN[h][0], C - 128), RUN[h][1]
+            q, s = V("zq" + h, 0, b - a), V("zs" + h, 0, b - a)
+            quant(q, s, V("zt", 4 * a, 4 * b))
+            for t in PEORDER[h]:
+                w = (128 * t, 128 * t + 128)
+                mm(made(h, t, a), V("wq", *w), V("wp", *w), q, s)
+
+        def leave():
+            quant(hq, hs, V("hf"))
+            send(far, lq, hq, "a_q" + R, 0, 16, codes=True)
+            send(far, lsc, hs, "a_s" + R, 0, 16)
+
+        def unpack():
+            for t in range(4):
+                e = (128 * t, 128 * t + 128)
+                mm(V("psB", 512 * t, 512 * t + HALF), V("eq", *e), V("es", *e), lq, lsc)
+
+        def product(h):
+            u = "v" if r == 3 else "u"
+            mm(score(h), V(u + "q"), V(u + "s"), *xq(h))
+
+        def packed(h, queues):
+            a, b = RUN[h]
+            q, s = xq(h)
+            store("y", T.oc[:, 4 * a:4 * b], q[0].bitcast(dt.uint8), q[1])
             for k in range(4):
-                store("y", T.osc[4 * k:4 * k + 4, HALF:C], T.xs[32 * k:32 * k + 4, HALF:C], xso[1])
-            mm(V("psA", 0, HALF), V("vq"), V("vs"), xqo, xso)
-            cp("s", V("yo", HALF, C), V("psA", 0, HALF))
-            store("y", T.y[:, HALF:C], V("yo", HALF, C)[0], V("yo", HALF, C)[1])
-            cp("s", V("pout", 0, C), pick(V("idf"), L(yk)))
-            cp("s", V("pout", C, 2 * C), pick(V("idf"), V(tu, 60, 80)))
+                store(queues[k % 2], T.osc[4 * k:4 * k + 4, a:b], T.xs[32 * k:32 * k + 4, a:b], s[1])
+
+        def result(h, q, dq):
+            o = V("yo", *RUN[h])
+            cp(q, o, score(h))
+            store(dq, T.y[:, RUN[h][0]:RUN[h][1]], o[0], o[1])
+
+        def lists():
+            cp("s", V("pout", 0, C), P16("yb"), bias=float(HALF))
+            cp("s", V("pout", C, 2 * C), pick(V("idn"), L(tu, 96)), bias=float(HALF))
             store("y", T.pl[:, :], T.pout[0:128:16, :], V("pout")[1])
 
-        for t in range(4):
-            e = (128 * t, 128 * t + 128)
-            mm(V("psB", 512 * t, 512 * t + HALF), V("eq", *e), V("es", *e), lq, lsc)
-        if r == 1:
-            mm(V("psA", 0, HALF), V("uq"), V("us"), xqo, xso)
-        for t in range(4):
-            o = V("xi", t, 4 * HALF, 4)
-            tt(o, V("psB", 512 * t, 512 * t + HALF), o, add)
-        if r < 3:
-            tt(V("df", 0, 20), L("pe"), V("bs", 0, 20), sub)
-        xqf, xsf = V("xq", 0, HALF), V("xs", 0, HALF)
-        quant(xqf, xsf, V("xi", 0, 4 * HALF))
-        if r < 3:
-            mm(V("psA", 512, 512 + HALF), V("uq"), V("us"), xqf, xsf)
-        else:
-            mm(V("psA", 512, 512 + HALF), V("vq"), V("vs"), xqf, xsf)
-            store("y", T.oc[:, 0:4 * HALF], xqf[0].bitcast(dt.uint8), xqf[1])
-            for k in range(4):
-                store("ys"[k % 2], T.osc[4 * k:4 * k + 4, 0:HALF], T.xs[32 * k:32 * k + 4, 0:HALF], xsf[1])
-            cp("v", V("yo", 0, HALF), V("psA", 512, 512 + HALF))
-            store("s", T.y[:, 0:HALF], V("yo", 0, HALF)[0], V("yo", 0, HALF)[1])
+        s = {
+            "uP": lambda: cp("v", L("uP"), L("iP")), "uE": lambda: cp("v", L("uE"), L("iE")),
+            "uF": lambda: cp("v", uF, L("iFY")), "uY": lambda: cp("v", uY, L("iFY", 20)),
+            "sendP": lambda: send(far, L("lp1"), L("uP"), "a_p1", 0, 4),
+            "po": lambda: cp("s", V("po"), pick(V("idn"), L("uP"))),
+            "pE": lambda: cp("s", P16("cb"), pick(V("po"), L("uE"))),
+            "iM": lambda: tt(L("iM"), L("iE"), L("cw"), AluOpType.min), "uM": lambda: cp("v", L("uM"), L("iM")),
+            "bP": lambda: ts(W("bs1", 1), V("iP"), -float(HALF), add),
+            "d0": lambda: tt(W("df1", 0), V("iE"), V("cw"), sub), "d1": lambda: tt(W("df1", 1), pick(V("tcb"), off(0)), W("bs1", 1), sub),
+            "ya": lambda: tt(V("ya"), pick(V("id0"), uY), V("idk"), add),
+            "wd": moved, "uFY": lambda: cp("v", V("uFY", 0, 40), V("iFY")), "off": lambda: ts(V("off", 0, 8), V("i8"), c1("f2"), add, 2.0 * C + 31, AluOpType.min),
+            "ofa": lambda: ts(V("off", 8, 12), V("i8", 0, 4), c1("fa"), add, 415.0, AluOpType.min),
+            "ofb": lambda: ts(V("off", 12, 16), V("i8", 0, 4), c1("fb"), add, 287.0, AluOpType.min),
+            "c2": lambda: tt(W("tb", 2), pick(V("tnm"), off(2)), V("cw"), add), "k2": lambda: cp("v", W(tu, 2), W("tb", 2)),
+            "p1": lambda: tt(W("pr", 1), pick(V("tnm"), off(1)), W(df, 1), mul),
+            "b1": lambda: tt(W("tb", 1), W("pr", 1), W(bs, 1), add), "l1": lambda: ts(W(tu, 1), W("tb", 1), float(HALF), add),
+            "pz": lambda: tt(W("pr", 0), pick(V("tnm"), off(0)), W(df, 0), mul),
+            "bz": lambda: tt(W("tb", 0), W("pr", 0), W(bs, 0), add), "lz": lambda: ts(W(tu, 0), W("tb", 0), float(HALF), add),
+            "yd": lambda: cp("s", V("yd"), pick(V("yc"), uF)),
+            "uq": lambda: quant(V("uq"), V("us"), V("ut")), "vq": lambda: quant(V("vq"), V("vs"), V("vt")), "later": later,
+            "p2": lambda: tt(W("pr", 2), pick(V("tnm"), off(2)), W("df1", 0), mul),
+            "b2": lambda: tt(W("tb", 2), W("pr", 2), W("bs1", 0), add), "l2": lambda: ts(W(tu, 2), W("tb", 2), float(HALF), add),
+            "p0": lambda: tt(W("pr", 0, 2), pick(V("tnm"), off(0, 2)), V(df), mul),
+            "b0": lambda: tt(W("tb", 0, 2), W("pr", 0, 2), V(bs), add), "l0": lambda: ts(W(tu, 0, 2), W("tb", 0, 2), float(HALF), add),
+            "p3": lambda: tt(W("pr", 3), pick(V("tnm"), off(3)), W(df, 1), mul),
+            "b3": lambda: tt(W(nbs, 1), W("pr", 3), W(bs, 1), add), "l3": lambda: ts(W(tu, 3), W(nbs, 1), float(HALF), add),
+            "sendB": lambda: send(partner[r], V(lp), W(tu, 3), "a_p" + N, 0, 8),
+            "y3": lambda: wrapped(W("y31", 0, 2), "cc", 0, 2) if r == 1 else wrapped(W("y3" + R, 0), "cc", 0),
+            "yf": lambda: cp("s", P16("yf"), pick(P16("yb"), uF)),
+            "wY": lambda: wrapped(W(yk, 0), "yb", 0), "wK": lambda: wrapped(W(yk, 1), "yb", 1), "wG": lambda: wrapped(V(yg), "yf", 0),
+            "sendK": lambda: send(far, kl, V(yk, 32, 42), "a_k" + R, *((8, 16) if r == 1 else (0, 8))),
+            "qa": lambda: layer("a"), "qb": lambda: layer("b"), "hq": leave, "un": unpack,
+            "cb": lambda: cp("s", P16("cb"), pick(V("cb", 0, C), L("uE"))),
+            "cc": lambda: cp("s", P16("cc"), pick(P16("yb"), L("y31", 32)) if again("cc") else pick(V("yd"), uF)),
+            "t2": lambda: cp("s", V("t2"), W("pr", 3), scale=-2.0), "dP": lambda: tt(W(ndf, 1), W(df, 1), V("t2"), add),
+            "bF": lambda: ts(W(nbs, 0), V(lp), -float(HALF), add),
+            "dF": lambda: tt(W(ndf, 0), pick(V("tcb"), off(0)), W(nbs, 0), sub),
+            "on": lambda: packed("n", "yy"), "of": lambda: packed("f", "ys"), "pl": lists,
+            "yn": lambda: result("n", "s", "y"), "yo": lambda: result("f", "v", "s"),
+        }
+        chain = {"g1": ("g1", 0, V("cb", 0, C if r == 1 else 2 * C + 16), tu, 64), "g2": ("g2", 0, V("g1"), tu, 32),
+                 "g4": ("g4", 0, V("g2"), "lp1", 0), "g3": ("g3", 0, V("g4" if r == 1 else "g2"), tu, 0),
+                 "yb": ("yb", 16, V("g3"), "y3" + R, 0), "yh": ("yf", 16, P16("yb"), "uFY", 0),
+                 "yc": ("yc", 0, V("ya"), "uFY", 0)}
+
+        def call(name):
+            n, _, cut = name.partition(":")
+            if n == "pq":
+                return shared("cb", 0, V("id0"), lp if again(n) else "lp1", 0, int(cut))
+            if n == "nm":
+                o, i = V("nm", 16 + HALF, 16 + C), pick(V("sg"), V("uM", 10, 20))
+                if r == 1:
+                    ts(V("nm", 16, 16 + HALF), pick(V("sg"), V("uM", 0, 10)), 0.0, less)
+                    return run("s", lambda: g.scalar.activation(o[0], i[0], ActivationFunctionType.Relu, scale=-1.0), [o], [i])
+                ts(V("nm", 16, 16 + HALF), pick(V("sg"), V("uM", 0, 10)), 0.0, less, c1("mv"), mul)
+                return run("s", lambda: g.scalar.activation(o[0], i[0], ActivationFunctionType.Relu, scale=c1("ms")[0]), [o], [i, c1("ms")])
+            if n in chain:
+                return shared(*chain[n], int(cut) if cut else HALF)
+            if n in s:
+                return s[n]()
+            if n[:2] in PADDED:
+                return turn(n[:2], n[2:])
+            if n[0] == "w" and len(n) == 3:
+                return part(*{"Y": (yk, 0, "yb", 0), "K": (yk, 32, "yb", 1), "G": (yg, 0, "yf", 0)}[n[1]], n[2])
+            if n[0] == "F":
+                a, b = ((0, 224), (224, C))[int(n[1])]
+                return cp(n[2], V("yf", 16 + a, 16 + b), pick(P16("yb"), V("uFY", a // 16, b // 16)))
+            if n[1] in "nf":
+                a, b = RUN[n[1]]
+                if n[0] == "q":
+                    return quant(*xq(n[1]), V("xi", 4 * a, 4 * b))
+                if n[0] == "m":
+                    return product(n[1])
+                o, i = V("sg", a, b), score(n[1])
+                if n[2] == "v":
+                    return ts(o, i, 0.0, less, -1.0, mul)
+                return run("s", lambda: g.scalar.activation(o[0], i[0], ActivationFunctionType.Sign), [o], [i])
+            t = int(n[1])
+            if n[0] == "e":
+                e = (128 * t, 128 * t + 128)
+                return quant(V("eq", *e), V("es", *e), V("et", 3 - t, 515 - t))
+            if n[0] == "n":
+                o = mixed("xi", t, HALF, C)
+                return tt(o, pick(row("hg", t), V(yk, 42, 52)), o, add)
+            if n[0] == "a":
+                o = mixed("xi", t, 0, HALF)
+                return tt(o, V("psB", 512 * t, 512 * t + HALF), o, add)
+            if n[0] == "f":
+                return cp(n[2], mixed("hf", t, 0, HALF), pick(row("hg", t), kl))
+            a, b = RUN[n[2]]
+            if n[0] == "X":
+                return cp(n[3], row("xg", t, a, b), mixed("xi", t, a, b), scale=0.5)
+            f = 0 if n[2] == "a" else 16
+            if n[0] == "A":
+                return cp(n[3:] or "s", row("ag", t, a, b), pick(row("xg", t), V(yk, f, f + (b - a) // 16)))
+            if n[0] == "Z":
+                return tt(mixed("zt", t, a, b), pick(row("xg", t), V(yg, f, f + (b - a) // 16)), row("ag", t, a, b), add)
+            cp(n[3], row("hg", t, a, b), made(n[2], t, a), scale=0.03125)
+
+        for name in ROUNDS[r - 1].split():
+            call(name)
+
+    for r in (1, 2, 3):
+        calls(r)
 
     for s in ["c_v", "c_s", "c_t", "c_g"] + ARRIVALS + ["sent", "stored"]:
         g.wait_ge(T.sem[s], count[s])
     for s in LOADS:
         g.wait_ge(T.sem[s], 16)
+
+
+PEORDER = {"a": (0, 2, 1, 3), "b": (0, 2, 1, 3)}

@@ -6,16 +6,22 @@ CUT = 192
 RUN = {"a": (0, CUT), "b": (CUT, C), "f": (0, HALF), "n": (HALF, C), "w": (0, C)}
 
 LOADORDER = "y:pb s:lg y:fd s:ex y:u s:x0 y:x1"
-FIRST = ("uFY uE uP sendP po ya yc:0 wd qf pE uq iM mf qn later uM d0 e0 off sfv mn snv bP X0wv nm cb0 cb1 yd cc nm1 nm0 d1 p2 p0 b2 p3 "
-         "b0 l2 pq:128 l0 cc1 cc0 g1 y3 g2 ofa ofb g4 b3 g3 l3 sendB X1wv yb X2wv ")
-SIGNS = "cc0 cc1 sfv nm y3 nm0 nm1 c2 p1 pz k2 b1 bz g1:96 l1 lz g2 p3 g3 b3 yb l3 sendB "
-LAYER = ("F0s F1s yb0a yb1a yb0b yb1b wYa yf0a yf1a wYb yf0b yf1b wGa wKa sendK wGb A0a A1a A2a A3a A0b A1b A2b A3b "
+IDQ = "vv"
+FIRST = ("zE zP i16 idn m0 m1 f16 par id0 idk cw bc f1 uFY uP sendP pads po uE ga gb ya uq yc:0 wd qf qn mf mn later pE iM d0 X0wv f2 uM "
+         "sfv snv off bP nm cb0 cb1 nm0 nm1 yd cc d1 e0 p2 p0 m2 p3 b2 b0 pq:128 l2 mv cc0 l0 g1 fa fb g2 X1wv cc1 g4 y3 g3 ofa ofb b3 "
+         "yb X2wv l3 sendB ")
+SIGNS = "sfv ub1 nm bF nm0 nm1 nz:32 dF c2 p1 nz0 k2 nz1 b1 g1:128 pz l1 bz g2:128 lz p3 yb b3 "
+LAYER = ("F0s F1s yb0a yb1a yb0b yb1b wYa yf0a yf1a yf0b yf1b wYb wGa wKa sendK wGb A0a A1a A2a A3a A0b A1b A2b A3b "
          "Z0a Z1a Z2a Z3a Z0b qa Z1b Z2b Z3b wKb qb "
-         "H0as H2as H1as H3av H0bv H2bv H1bs f0v f2s H3bv f3v f1s hq ")
-FLIGHT = "n0 n1 n2 n3 qn pq:0 cb t2 cc X0ns X1ns X2ns X3ns mn sns bF cb0 cb1 dP un a0 a1 a2 a3 dF qf X0fs X1fs X2fs X3fs mf "
-LAST = "n0 n1 n2 n3 qn vq on mn pl yn un a0 a1 a2 a3 qf mf of yo"
-ROUNDS = (FIRST + LAYER.replace("A0a", "X3wv A0a").replace("qb", "e1 qb").replace("H3av", "H3av e2").replace("hq", "e3 hq") + FLIGHT,
-          SIGNS + LAYER + FLIGHT, SIGNS.replace("sendB ", "") + LAYER + LAST)
+         "H0as H2as H1as H3av H0bv H2bv H1bs H3bv f0v f2s f3v f1s hq ")
+FLIGHT = "t2 pq:0 cb ua ub n0 n1 n2 n3 dP X0nv X1nv X2nv qn X3nv un mn sns a0 a1 a2 a3 ua0 qf X0fs X1fs X2fs X3fs mf ua1 ub0 "
+SHORT = "t2 pq:0 cb ua ub n0 n1 n2 n3 e2 e3 qn dP un mn sns a0 a1 a2 a3 ua0 qf X0ws X1ws X2fs X2nv mf ua1 ub0 X3wv "
+LAST = "pl n0 n1 n2 n3 qn on un mn yn a0 a1 a2 a3 qf mf of yo"
+EARLY = LAYER.replace("H0as", "cc H0as").replace("H3av", "H3as cc0 cc1").replace("hq", "y3n hq")
+ROUNDS = (FIRST + EARLY.replace("A0a", "X3wv A0a").replace("qb", "e1 qb") + SHORT,
+          SIGNS + EARLY.replace("wYa", "l3 sendB wYa") + FLIGHT, SIGNS + LAYER.replace("wYa", "l3 wYa").replace("hq", "vq hq") + LAST)
+
+WSRC, WDST = "yc", "id0"
 
 SCRATCH = {
     "xi": ("sbuf", [128, 4 * C], "bfloat16"), "xg": ("sbuf", [128, 4 * C], "bfloat16"),
@@ -52,10 +58,13 @@ SCRATCH = {
     "bs4": ("sbuf", [128, 64], "float32"),
 }
 PADDED = ("cb", "nm", "cc", "yb", "yf")
-for _n in PADDED:
+LATER = ("ua", "ub", "nz")
+for _n in PADDED + LATER:
     SCRATCH[_n] = ("sbuf", [128, C + 32], "bfloat16")
+for _n in LATER:
+    SCRATCH["t" + _n] = ("sbuf", [128, 2 * C + 32], "bfloat16")
 SCRATCH["cb"] = ("sbuf", [128, 2 * C + 32], "bfloat16")
-for _n in ("fa", "fb", "m2", "mv", "ms"):
+for _n in ("fa", "fb", "m2", "mv", "ga", "gb"):
     SCRATCH[_n] = ("sbuf", [128, 8], "float32")
 TURNS = {"0": (0, 0, C + 32), "1": (C + 32, 16, C), "0a": (0, 0, 224), "1a": (224, 16, 192), "0b": (416, 192, 160), "1b": (576, 208, 128)}
 for _r in "123":
@@ -243,45 +252,41 @@ def rank_program(g, core, T, topo):
         load("y", V("vt"), T.v[:, :], "d_v")
 
     def moved():
-        order("y", V("yc")[1], V("id0")[1])
-        g.sync.dma_start(T.id0[1:128:16, :], T.yc[1:128:16, :]).then_inc(T.sem.d_wf, 16)
-        note(("d_wf", 16, {"d_wf": 16}), V("yc")[1], V("id0")[1])
+        order("y", V(WSRC)[1], V(WDST)[1])
+        g.sync.dma_start(T[WDST][1:128:16, :], T[WSRC][1:128:16, :]).then_inc(T.sem.d_wf, 16)
+        note(("d_wf", 16, {"d_wf": 16}), V(WSRC)[1], V(WDST)[1])
 
     def iota(out, pattern, base, cm):
         run("g", lambda: g.iota(out[0], pattern, base, cm), [out], [])
 
+    def pads():
+        for n in PADDED + LATER:
+            for a in (C, 2 * C + 16) if n == "cb" else (0, 16 + C):
+                o = V(n, a, a + 16)
+                run("g", lambda: g.iota(o[0], [[0, 16]], 0, 0, allow_small_or_imprecise_dtypes=True), [o], [])
+
     iota(c1("i17"), [[0, 1]], 0, 17)
     iota(V("ik"), [[16, 32]], 0, 0)
+    iota(V("i8"), [[1, 4], [256, 2]], 0, 0)
     fill(V("ones"), 1.0)
     o, i = V("et"), V("ones")
     run("g", lambda: g.affine_select(o[0], i[0], [[1, 516]], AluOpType.is_equal, 0.0, -3, -4), [o], [i])
-    iota(V("i8"), [[1, 4], [256, 2]], 0, 0)
 
-    ts(c1("i16"), c1("i17"), 15, AluOpType.bitwise_and)
-    ts(c1("par"), c1("i17"), 4, AluOpType.logical_shift_right, 1, AluOpType.bitwise_and)
     d, one = V("idn"), V("ones", 0, C)
-    run("v", lambda: g.vector.tensor_tensor_scan(d[0], one[0], one[0], -HALF - 1.0, mul, add), [d], [one])
-    ts(c1("m0"), c1("i16"), 1.0, AluOpType.not_equal)
-    ts(c1("m1"), c1("i16"), 1.0, AluOpType.is_equal)
-    ts(c1("f1"), c1("par"), -336.0, mul, 352.0, add)
-    cp("v", c1("f16"), c1("i16"))
-    fill(V("iP", 20, 32), 0)
-    ts(c1("f2"), c1("i16"), 16.0, mul, c1("f1"), add)
-    ts(V("cw"), V("ik"), c1("f16"), add)
-    ts(W("bs1", 0), V("ik"), c1("f16"), add, -float(HALF), add)
-    fill(V("iE", 20, 32), 0)
-    ts(c1("fa"), c1("par"), 128.0, mul, -128.0, add)
-    ts(c1("fb"), c1("par"), 192.0, mul, -192.0, add)
-    ts(c1("m2"), c1("i16"), 2.0, AluOpType.is_equal, C + 15.0, mul)
-    tt(c1("fa"), c1("fa"), c1("f2"), add)
-    tt(c1("fb"), c1("fb"), c1("f2"), add)
-    ts(c1("mv"), c1("m2"), 1.0, add)
-    ts(c1("ms"), c1("m2"), 1.0, add, -1.0, mul)
-    cp("s", V("id0"), V("idn"), scale=c1("m0"))
-    cp("s", V("idk"), V("idn"), scale=c1("m1"))
-    for n in PADDED:
-        for a in (C, 2 * C + 16) if n == "cb" else (0, 16 + C):
-            cp("s", V(n, a, a + 16), V("ones", 0, 16))
+    constants = {
+        "i16": lambda: ts(c1("i16"), c1("i17"), 15, AluOpType.bitwise_and),
+        "par": lambda: ts(c1("par"), c1("i17"), 4, AluOpType.logical_shift_right, 1, AluOpType.bitwise_and),
+        "idn": lambda: run("v", lambda: g.vector.tensor_tensor_scan(d[0], one[0], one[0], -HALF - 1.0, mul, add), [d], [one]),
+        "m0": lambda: ts(c1("m0"), c1("i16"), 1.0, AluOpType.not_equal), "m1": lambda: ts(c1("m1"), c1("i16"), 1.0, AluOpType.is_equal),
+        "id0": lambda: cp(IDQ[0], V("id0"), V("idn"), scale=c1("m0")), "idk": lambda: cp(IDQ[1], V("idk"), V("idn"), scale=c1("m1")),
+        "f1": lambda: ts(c1("f1"), c1("par"), -336.0, mul, 352.0, add), "f2": lambda: ts(c1("f2"), c1("i16"), 16.0, mul, c1("f1"), add),
+        "ga": lambda: ts(c1("ga"), c1("par"), -208.0, mul, 224.0, add), "fa": lambda: ts(c1("fa"), c1("i16"), 16.0, mul, c1("ga"), add),
+        "gb": lambda: ts(c1("gb"), c1("par"), -144.0, mul, 160.0, add), "fb": lambda: ts(c1("fb"), c1("i16"), 16.0, mul, c1("gb"), add),
+        "f16": lambda: cp("v", c1("f16"), c1("i16")), "cw": lambda: ts(V("cw"), V("ik"), c1("f16"), add),
+        "bc": lambda: ts(W("bs1", 0), V("ik"), c1("f16"), add, -float(HALF), add),
+        "zP": lambda: fill(V("iP", 20, 32), 0), "zE": lambda: fill(V("iE", 20, 32), 0),
+        "m2": lambda: ts(c1("m2"), c1("i16"), 2.0, AluOpType.is_equal, C + 15.0, mul), "mv": lambda: ts(c1("mv"), c1("m2"), 1.0, add),
+    }
 
     def calls(r):
         R, N = str(r), str(r + 1)
@@ -357,7 +362,7 @@ def rank_program(g, core, T, topo):
             "c2": lambda: tt(W("tb", 2), pick(V("tnm"), off(2)), V("cw"), add), "k2": lambda: cp("v", W(tu, 2), W("tb", 2)),
             "p1": lambda: tt(W("pr", 1), pick(V("tnm"), off(1)), W(df, 1), mul),
             "b1": lambda: tt(W("tb", 1), W("pr", 1), W(bs, 1), add), "l1": lambda: ts(W(tu, 1), W("tb", 1), float(HALF), add),
-            "pz": lambda: tt(W("pr", 0), pick(V("tnm"), off(0)), W(df, 0), mul),
+            "pz": lambda: tt(W("pr", 0), pick(V("tnz"), off(0)), W(df, 0), mul),
             "bz": lambda: tt(W("tb", 0), W("pr", 0), W(bs, 0), add), "lz": lambda: ts(W(tu, 0), W("tb", 0), float(HALF), add),
             "yd": lambda: cp("s", V("yd"), pick(V("yc"), uF)),
             "uq": lambda: quant(V("uq"), V("us"), V("ut")), "vq": lambda: quant(V("vq"), V("vs"), V("vt")), "later": later,
@@ -376,32 +381,39 @@ def rank_program(g, core, T, topo):
             "cb": lambda: cp("s", P16("cb"), pick(V("cb", 0, C), L("uE"))),
             "cc": lambda: cp("s", P16("cc"), pick(P16("yb"), L("y31", 32)) if again("cc") else pick(V("yd"), uF)),
             "t2": lambda: cp("s", V("t2"), W("pr", 3), scale=-2.0), "dP": lambda: tt(W(ndf, 1), W(df, 1), V("t2"), add),
-            "bF": lambda: ts(W(nbs, 0), V(lp), -float(HALF), add),
-            "dF": lambda: tt(W(ndf, 0), pick(V("tcb"), off(0)), W(nbs, 0), sub),
+            "y3n": lambda: wrapped(W("y3" + N, 0), "cc", 0),
+            "ua": lambda: cp("s", P16("ua"), pick(V("cb", 0, C), L("y3" + N))),
+            "ub": lambda: cp("s", P16("ub"), pick(P16("cb"), L("y3" + N))),
+            "nz": lambda: cp("s", P16("nz"), pick(P16("nm"), L("y3" + R))),
+            "bF": lambda: cp("v", W(bs, 0), pick(V("tua"), off(0))),
+            "dF": lambda: tt(W(df, 0), pick(V("tub"), off(0)), W(bs, 0), sub),
+            "pads": pads,
             "on": lambda: packed("n", "yy"), "of": lambda: packed("f", "ys"), "pl": lists,
             "yn": lambda: result("n", "s", "y"), "yo": lambda: result("f", "v", "s"),
         }
         chain = {"g1": ("g1", 0, V("cb", 0, C if r == 1 else 2 * C + 16), tu, 64), "g2": ("g2", 0, V("g1"), tu, 32),
-                 "g4": ("g4", 0, V("g2"), "lp1", 0), "g3": ("g3", 0, V("g4" if r == 1 else "g2"), tu, 0),
-                 "yb": ("yb", 16, V("g3"), "y3" + R, 0), "yh": ("yf", 16, P16("yb"), "uFY", 0),
-                 "yc": ("yc", 0, V("ya"), "uFY", 0)}
+                 "g4": ("g4", 0, V("g2"), "lp1", 0), "g3": ("g3", 0, V("g4"), tu, 0),
+                 "yb": ("yb", 16, V("g3"), "y31", 0) if r == 1 else ("yb", 16, V("g2"), tu, 0), "yh": ("yf", 16, P16("yb"), "uFY", 0),
+                 "yc": ("yc", 0, V("ya"), "uFY", 0), "nz": ("nz", 16, P16("nm"), "y3" + R, 0)}
 
         def call(name):
             n, _, cut = name.partition(":")
             if n == "pq":
-                return shared("cb", 0, V("id0"), lp if again(n) else "lp1", 0, int(cut))
+                return shared("cb", 0, V(WDST), lp if again(n) else "lp1", 0, int(cut))
             if n == "nm":
                 o, i = V("nm", 16 + HALF, 16 + C), pick(V("sg"), V("uM", 10, 20))
                 if r == 1:
-                    ts(V("nm", 16, 16 + HALF), pick(V("sg"), V("uM", 0, 10)), 0.0, less)
-                    return run("s", lambda: g.scalar.activation(o[0], i[0], ActivationFunctionType.Relu, scale=-1.0), [o], [i])
-                ts(V("nm", 16, 16 + HALF), pick(V("sg"), V("uM", 0, 10)), 0.0, less, c1("mv"), mul)
-                return run("s", lambda: g.scalar.activation(o[0], i[0], ActivationFunctionType.Relu, scale=c1("ms")[0]), [o], [i, c1("ms")])
+                    ts(V("nm", 16, 16 + HALF), pick(V("sg"), V("uM", 0, 10)), 0.0, AluOpType.max)
+                    return run("s", lambda: g.scalar.activation(o[0], i[0], ActivationFunctionType.Relu), [o], [i])
+                ts(V("nm", 16, 16 + HALF), pick(V("sg"), V("uM", 0, 10)), 0.0, AluOpType.max, c1("mv"), mul)
+                return run("s", lambda: g.scalar.activation(o[0], i[0], ActivationFunctionType.Relu, scale=c1("mv")[0]), [o], [i, c1("mv")])
+            if n in constants:
+                return constants[n]()
             if n in chain:
                 return shared(*chain[n], int(cut) if cut else HALF)
             if n in s:
                 return s[n]()
-            if n[:2] in PADDED:
+            if n[:2] in PADDED + LATER:
                 return turn(n[:2], n[2:])
             if n[0] == "w" and len(n) == 3:
                 return part(*{"Y": (yk, 0, "yb", 0), "K": (yk, 32, "yb", 1), "G": (yg, 0, "yf", 0)}[n[1]], n[2])
@@ -416,8 +428,8 @@ def rank_program(g, core, T, topo):
                     return product(n[1])
                 o, i = V("sg", a, b), score(n[1])
                 if n[2] == "v":
-                    return ts(o, i, 0.0, less, -1.0, mul)
-                return run("s", lambda: g.scalar.activation(o[0], i[0], ActivationFunctionType.Sign), [o], [i])
+                    return ts(o, i, 0.0, less)
+                return run("s", lambda: g.scalar.activation(o[0], i[0], ActivationFunctionType.Sign, scale=-1.0), [o], [i])
             t = int(n[1])
             if n[0] == "e":
                 e = (128 * t, 128 * t + 128)
@@ -446,10 +458,10 @@ def rank_program(g, core, T, topo):
     for r in (1, 2, 3):
         calls(r)
 
-    for s in ["c_v", "c_s", "c_t", "c_g"] + ARRIVALS + ["sent", "stored"]:
-        g.wait_ge(T.sem[s], count[s])
     for s in LOADS:
         g.wait_ge(T.sem[s], 16)
+    for s in ["c_g"] + ARRIVALS + ["sent", "c_t", "c_s", "c_v", "stored"]:
+        g.wait_ge(T.sem[s], count[s])
 
 
 PEORDER = {"a": (0, 2, 1, 3), "b": (0, 2, 1, 3)}

from concourse.mybir import dt, AluOpType, ActivationFunctionType

C, HALF = 320, 160
MASKS = (1, 2, 4)
CUT = 192
RUN = {"a": (0, CUT), "b": (CUT, C), "f": (0, HALF), "n": (HALF, C), "w": (0, C)}

LOADORDER = "y:pb s:lg y:fd s:ex y:u s:x0 y:x1"
IDQ = "vv"
FIRST = ("zE zP i16 idn m0 m1 f16 par id0 idk cw bc f1 uFY uP sendP pads po uE ga gb ya uq yc:0 wd qf qn mf mn later pE iM d0 X0wv f2 uM "
         "sfv snv off bP nm cb0 cb1 nm0 nm1 yd cc d1 e0 p2 p0 m2 p3 b2 b0 pq:128 l2 mv cc0 l0 g1 fa fb g2 X1wv cc1 g4 y3 g3 ofa ofb b3 "
         "yb X2wv l3 sendB ")
SIGNS = "sfv ub1 nm bF nm0 nm1 nz:32 dF c2 p1 nz0 k2 nz1 b1 g1:128 pz l1 bz g2:128 lz p3 yb b3 "
LAYER = ("F0s F1s yb0a yb1a yb0b yb1b wYa yf0a yf1a yf0b yf1b wYb wGa wKa sendK wGb A0a A1a A2a A3a A0b A1b A2b A3b "
         "Z0a Z1a Z2a Z3a Z0b qa Z1b Z2b Z3b wKb qb "
         "H0as H2as H1as H3av H0bv H2bv H1bs H3bv f0v f2s f3v f1s hq ")
FLIGHT = "t2 pq:0 cb ua ub n0 n1 n2 n3 dP X0nv X1nv X2nv qn X3nv un mn sns a0 a1 a2 a3 ua0 qf X0fs X1fs X2fs X3fs mf ua1 ub0 "
SHORT = "t2 pq:0 cb ua ub n0 n1 n2 n3 e2 e3 qn dP un mn sns a0 a1 a2 a3 ua0 qf X0ws X1ws X2fs X2nv mf ua1 ub0 X3wv "
LAST = "pl n0 n1 n2 n3 qn on un mn yn a0 a1 a2 a3 qf mf of yo"
EARLY = LAYER.replace("H0as", "cc H0as").replace("H3av", "H3as cc0 cc1").replace("hq", "y3n hq")
ROUNDS = (FIRST + EARLY.replace("A0a", "X3wv A0a").replace("qb", "e1 qb") + SHORT,
          SIGNS + EARLY.replace("wYa", "l3 sendB wYa") + FLIGHT, SIGNS + LAYER.replace("wYa", "l3 wYa").replace("hq", "vq hq") + LAST)

WSRC, WDST = "yc", "id0"

SCRATCH = {
    "xi": ("sbuf", [128, 4 * C], "bfloat16"), "xg": ("sbuf", [128, 4 * C], "bfloat16"),
    "ag": ("sbuf", [128, 4 * C], "bfloat16"), "zt": ("sbuf", [128, 4 * C], "bfloat16"),
    "hg": ("sbuf", [128, 4 * C], "bfloat16"), "hf": ("sbuf", [128, 4 * HALF], "bfloat16"),
    "ut": ("sbuf", [128, 512], "bfloat16"), "vt": ("sbuf", [128, 512], "bfloat16"),
    "ones": ("sbuf", [128, 516], "bfloat16"), "et": ("sbuf", [128, 516], "bfloat16"),
    "uq": ("sbuf", [128, 128], "float8_e4m3fn_x4"), "us": ("sbuf", [128, 128], "uint8"),
    "vq": ("sbuf", [128, 128], "float8_e4m3fn_x4"), "vs": ("sbuf", [128, 128], "uint8"),
    "wq": ("sbuf", [128, 512], "float8_e4m3fn_x4"), "wp": ("sbuf", [128, 512], "uint8"),
    "eq": ("sbuf", [128, 512], "float8_e4m3fn_x4"), "es": ("sbuf", [128, 512], "uint8"),
    "xq": ("sbuf", [128, C], "float8_e4m3fn_x4"), "xs": ("sbuf", [128, C], "uint8"),
    "zqa": ("sbuf", [128, C], "float8_e4m3fn_x4"), "zsa": ("sbuf", [128, C], "uint8"),
    "zqb": ("sbuf", [128, C], "float8_e4m3fn_x4"), "zsb": ("sbuf", [128, C], "uint8"),
    "iP": ("sbuf", [128, 32], "int32"), "iE": ("sbuf", [128, 32], "int32"), "iFY": ("sbuf", [128, 40], "int32"),
    "uP": ("sbuf", [128, 32], "uint16"), "uE": ("sbuf", [128, 32], "uint16"), "uFY": ("sbuf", [128, 48], "uint16"),
    "uM": ("sbuf", [128, 32], "uint16"), "off": ("sbuf", [128, 16], "uint16"),
    "i17": ("sbuf", [128, 8], "int32"), "ik": ("sbuf", [128, 32], "int32"), "i8": ("sbuf", [128, 8], "int32"),
    "i16": ("sbuf", [128, 8], "int32"), "par": ("sbuf", [128, 8], "int32"), "iM": ("sbuf", [128, 32], "float32"),
    "f1": ("sbuf", [128, 8], "float32"), "f2": ("sbuf", [128, 8], "float32"), "f16": ("sbuf", [128, 8], "float32"),
    "m0": ("sbuf", [128, 8], "float32"), "m1": ("sbuf", [128, 8], "float32"),
    "pr": ("sbuf", [128, 128], "float32"), "tb": ("sbuf", [128, 96], "float32"),
    "cw": ("sbuf", [128, 32], "float32"), "t2": ("sbuf", [128, 32], "float32"),
    "idn": ("sbuf", [128, C], "bfloat16"), "idk": ("sbuf", [128, C], "bfloat16"), "id0": ("sbuf", [128, C], "bfloat16"),
    "wf": ("sbuf", [128, C], "bfloat16"), "pp": ("sbuf", [128, C], "bfloat16"), "po": ("sbuf", [128, C], "bfloat16"),
    "sg": ("sbuf", [128, C], "bfloat16"), "g1": ("sbuf", [128, C], "bfloat16"), "g2": ("sbuf", [128, C], "bfloat16"),
    "g3": ("sbuf", [128, C], "bfloat16"), "g4": ("sbuf", [128, C], "bfloat16"), "ya": ("sbuf", [128, C], "bfloat16"),
    "yc": ("sbuf", [128, C], "bfloat16"), "yd": ("sbuf", [128, C], "bfloat16"),
    "tnm": ("sbuf", [128, 2 * C + 32], "bfloat16"), "tyb": ("sbuf", [128, 2 * C + 64], "bfloat16"),
    "tyf": ("sbuf", [128, 2 * C + 64], "bfloat16"), "tcb": ("sbuf", [128, 2 * C + 32], "bfloat16"),
    "tcc": ("sbuf", [128, 2 * C + 32], "bfloat16"),
    "yo": ("sbuf", [128, C], "float32"), "pout": ("sbuf", [128, 2 * C], "float32"),
    "psA": ("psum", [128, 2048], "float32"), "psB": ("psum", [128, 2048], "float32"),
    "bs4": ("sbuf", [128, 64], "float32"),
}
PADDED = ("cb", "nm", "cc", "yb", "yf")
LATER = ("ua", "ub", "nz")
for _n in PADDED + LATER:
    SCRATCH[_n] = ("sbuf", [128, C + 32], "bfloat16")
for _n in LATER:
    SCRATCH["t" + _n] = ("sbuf", [128, 2 * C + 32], "bfloat16")
SCRATCH["cb"] = ("sbuf", [128, 2 * C + 32], "bfloat16")
for _n in ("fa", "fb", "m2", "mv", "ga", "gb"):
    SCRATCH[_n] = ("sbuf", [128, 8], "float32")
TURNS = {"0": (0, 0, C + 32), "1": (C + 32, 16, C), "0a": (0, 0, 224), "1a": (224, 16, 192), "0b": (416, 192, 160), "1b": (576, 208, 128)}
for _r in "123":
    SCRATCH["lp" + _r] = ("sbuf", [128, 32], "uint16")
    SCRATCH["bs" + _r] = ("sbuf", [128, 64], "float32")
    SCRATCH["df" + _r] = ("sbuf", [128, 64], "float32")
    SCRATCH["tu" + _r] = ("sbuf", [128, 128], "uint16")
    SCRATCH["yk" + _r] = ("sbuf", [128, 64], "uint16")
    SCRATCH["yg" + _r] = ("sbuf", [128, 32], "uint16")
    SCRATCH["y3" + _r] = ("sbuf", [128, 64], "uint16")
    SCRATCH["kl" + _r] = ("sbuf", [128, 16], "uint16")
    SCRATCH["hq" + _r] = ("sbuf", [128, HALF], "float8_e4m3fn_x4")
    SCRATCH["hs" + _r] = ("sbuf", [128, HALF], "uint8")
    SCRATCH["lq" + _r] = ("sbuf", [128, HALF], "float8_e4m3fn_x4")
    SCRATCH["ls" + _r] = ("sbuf", [128, HALF], "uint8")

LOADS = ["d_pb", "d_ex", "d_fd", "d_lg", "d_x0", "d_x1", "d_u", "d_v", "d_wc", "d_ws", "d_wf"]
ARRIVALS = ["a_%s%d" % (k, r) for k in "pkqs" for r in (1, 2, 3)]
SEMAPHORES = ["c_v", "c_s", "c_t", "c_g", "sent", "stored"] + LOADS + ARRIVALS


def rank_program(g, core, T, topo):
    rank = T.rank_of(core)
    if rank is None:
        return
    queue = {"v": g.vector, "s": g.scalar, "t": g.tensor, "g": g, "y": g.sync}
    count = {"c_v": 0, "c_s": 0, "c_t": 0, "c_g": 0, "sent": 0, "stored": 0}
    known = {q: {} for q in queue}
    touched = {n: [] for n in SCRATCH}
    copy, ident = ActivationFunctionType.Copy, ActivationFunctionType.Identity
    add, sub, mul, less = AluOpType.add, AluOpType.subtract, AluOpType.mult, AluOpType.is_lt

    def meets(a, b):
        if a[1] <= b[0] or b[1] <= a[0]:
            return False
        if a[2] == b[2]:
            return (a[0] - b[0]) % a[2] == 0
        return True

    def order(q, reads, writes):
        deps = []
        for regs, w in ((reads, False), (writes, True)):
            for n, a, b, st in regs:
                for reg, wrote, op in touched[n]:
                    if (w or wrote) and meets((a, b, st), reg) and known[q].get(op[0], 0) < op[1]:
                        deps.append(op)
        want = {}
        for op in deps:
            if any(o is not op and o[2].get(op[0], 0) >= op[1] and not (o[0] == op[0] and o[1] == op[1]) for o in deps):
                continue
            want[op[0]] = max(want.get(op[0], 0), op[1])
        for s in want:
            queue[q].wait_ge(T.sem[s], want[s])
        for op in deps:
            for s, c in op[2].items():
                known[q][s] = max(known[q].get(s, 0), c)

    def note(op, reads, writes):
        for n, a, b, st in writes:
            if st == 1:
                touched[n][:] = [t for t in touched[n] if not (a <= t[0][0] and t[0][1] <= b)]
            touched[n].append(((a, b, st), True, op))
        for n, a, b, st in reads:
            touched[n].append(((a, b, st), False, op))

    def run(q, call, outs, ins):
        reads = [r for v in ins for r in v[1]]
        writes = [r for v in outs for r in v[1]]
        order(q, reads, writes)
        sem = "c_" + q
        count[sem] += 1
        call().then_inc(T.sem[sem], 1)
        clock = dict(known[q])
        clock[sem] = count[sem]
        note((sem, count[sem], clock), reads, writes)

    def V(n, a=0, b=None, st=1):
        b = SCRATCH[n][1][1] if b is None else b
        t = T[n]
        if SCRATCH[n][0] == "psum":
            return (t[:, a:b], [(n, 512 * (a // 512), 512 * (a // 512) + 512, 1)])
        return (t[:, a:b:st] if st > 1 else t[:, a:b], [(n, a, b, st)])

    def pick(win, off):
        return (win[0].indirect(off[0]), win[1] + off[1])

    def cp(q, out, in_, scale=None, bias=None):
        if q == "v" and scale is not None:
            ts(out, in_, scale, mul)
        elif q == "v":
            run(q, lambda: g.vector.tensor_copy(out[0], in_[0]), [out], [in_])
        elif isinstance(scale, tuple):
            run(q, lambda: g.scalar.activation(out[0], in_[0], copy, scale=scale[0]), [out], [in_, scale])
        elif scale is not None:
            run(q, lambda: g.scalar.activation(out[0], in_[0], copy, scale=scale), [out], [in_])
        elif bias is not None:
            run(q, lambda: g.scalar.activation(out[0], in_[0], ident, bias=bias), [out], [in_])
        else:
            run(q, lambda: g.scalar.activation(out[0], in_[0], copy), [out], [in_])

    def tt(out, a, b, op):
        run("v", lambda: g.vector.tensor_tensor(out[0], a[0], b[0], op), [out], [a, b])

    def ts(out, a, s1, op0, s2=None, op1=None):
        cols = [s for s in (s1, s2) if isinstance(s, tuple)]
        p1 = s1[0] if isinstance(s1, tuple) else s1
        p2 = s2[0] if isinstance(s2, tuple) else s2
        if op1 is None:
            run("v", lambda: g.vector.tensor_scalar(out[0], a[0], p1, None, op0), [out], [a] + cols)
        else:
            run("v", lambda: g.vector.tensor_scalar(out[0], a[0], p1, p2, op0, op1), [out], [a] + cols)

    def fill(out, value):
        run("v", lambda: g.vector.memset(out[0], value), [out], [])

    def quant(q, s, t):
        run("v", lambda: g.vector.quantize_mx(q[0], s[0], t[0]), [q, s], [t])

    def mm(out, w, ws, x, xs):
        run("t", lambda: g.tensor.matmul_mx(out[0], w[0], ws[0], x[0], xs[0], True, True), [out], [w, ws, x, xs])

    def load(q, out, src, sem, codes=False):
        order(q, [], out[1])
        ap = out[0].bitcast(dt.uint8) if codes else out[0]
        queue[q].dma_start(ap, src).then_inc(T.sem[sem], 16)
        note((sem, 16, {sem: 16}), [], out[1])

    def store(q, dst, src, regs):
        order(q, regs, [])
        queue[q].dma_start(dst, src).then_inc(T.sem.stored, 16)
        count["stored"] += 16

    def send(dst, out, in_, sem, lo, hi, codes=False):
        order("g", in_[1], [])
        es = topo.engines(core, dst)[lo:hi]
        rid, pid, _ = topo.addr(dst)
        o, i = (out[0].bitcast(dt.uint8), in_[0].bitcast(dt.uint8)) if codes else (out[0], in_[0])
        g.remote_dma(o, i, T.sem[sem], T.sem.sent, pid, rid, sum(1 << e for e in es))
        count["sent"] += len(es)
        n = len(topo.engines(dst, core)[lo:hi])
        count[sem] = n
        note((sem, n, {sem: n}), [], out[1])

    def turn(n, i):
        o, a, k = TURNS[i]
        a += C if n == "cb" else 0
        d, p = V("t" + n, o, o + k), V(n, a, a + k)
        run("v", lambda: g.vector.transpose(d[0], p[0]), [d], [p])

    def part(out, o, n, j, h):
        w, a = (V("t" + n, 0, 416), 0) if h == "a" else (V("t" + n, 416, 704), CUT // 16 if j else 16)
        f = 8 + 2 * j + (0 if h == "a" else 4)
        ts(V(out, o + a, o + a + 16), pick(w, V("off", f, f + 1)), float(HALF), add)

    def wrapped(out, n, j, k=1):
        ts(out, pick(V("t" + n, 0, 2 * C + 32), off(j, k)), float(HALF), add)

    def shared(out, o, win, offs, a, cut):
        if cut > 0:
            cp("v", V(out, o, o + cut), pick(win, V(offs, a, a + cut // 16)))
        if cut < C:
            cp("s", V(out, o + cut, o + C), pick(win, V(offs, a + cut // 16, a + 20)))

    c1 = lambda n: V(n, 0, 1)
    L = lambda n, a=0: V(n, a, a + 20)
    W = lambda n, j, k=1: V(n, 32 * j, 32 * (j + k))
    off = lambda j, k=1: V("off", 2 * j, 2 * (j + k))
    P16 = lambda n: V(n, C + 16, 2 * C + 16) if n == "cb" else V(n, 16, 16 + C)
    row = lambda n, t, a=0, b=C: V(n, C * t + a, C * t + b)
    mixed = lambda n, t, a, b: V(n, 4 * a + t, 4 * b, 4)
    partner = [T.cores[rank ^ m] for m in MASKS]
    uF, uY = L("uFY"), L("uFY", 20)

    first = {"pb": (L("iP"), T.pb[:, :]), "u": (V("ut"), T.u[:, :]), "ex": (L("iE"), T.ex[:, :]), "lg": (L("iFY", 20), T.lg[:, :]),
             "fd": (L("iFY"), T.fd[:, :]), "x0": (V("xi", 0, 4 * HALF), T.x[:, 0:4 * HALF]),
             "x1": (V("xi", 4 * HALF, 4 * C), T.x[:, 4 * HALF:4 * C])}
    for s in LOADORDER.split():
        q, n = s.split(":")
        load(q, first[n][0], first[n][1], "d_" + n)

    def later():
        order("y", V("xi")[1], [])
        load("y", V("wq"), T.wc[:, :], "d_wc", codes=True)
        load("y", V("wp"), T.ws[:, :], "d_ws")
        load("y", V("vt"), T.v[:, :], "d_v")

    def moved():
        order("y", V(WSRC)[1], V(WDST)[1])
        g.sync.dma_start(T[WDST][1:128:16, :], T[WSRC][1:128:16, :]).then_inc(T.sem.d_wf, 16)
        note(("d_wf", 16, {"d_wf": 16}), V(WSRC)[1], V(WDST)[1])

    def iota(out, pattern, base, cm):
        run("g", lambda: g.iota(out[0], pattern, base, cm), [out], [])

    def pads():
        for n in PADDED + LATER:
            for a in (C, 2 * C + 16) if n == "cb" else (0, 16 + C):
                o = V(n, a, a + 16)
                run("g", lambda: g.iota(o[0], [[0, 16]], 0, 0, allow_small_or_imprecise_dtypes=True), [o], [])

    iota(c1("i17"), [[0, 1]], 0, 17)
    iota(V("ik"), [[16, 32]], 0, 0)
    iota(V("i8"), [[1, 4], [256, 2]], 0, 0)
    fill(V("ones"), 1.0)
    o, i = V("et"), V("ones")
    run("g", lambda: g.affine_select(o[0], i[0], [[1, 516]], AluOpType.is_equal, 0.0, -3, -4), [o], [i])

    d, one = V("idn"), V("ones", 0, C)
    constants = {
        "i16": lambda: ts(c1("i16"), c1("i17"), 15, AluOpType.bitwise_and),
        "par": lambda: ts(c1("par"), c1("i17"), 4, AluOpType.logical_shift_right, 1, AluOpType.bitwise_and),
        "idn": lambda: run("v", lambda: g.vector.tensor_tensor_scan(d[0], one[0], one[0], -HALF - 1.0, mul, add), [d], [one]),
        "m0": lambda: ts(c1("m0"), c1("i16"), 1.0, AluOpType.not_equal), "m1": lambda: ts(c1("m1"), c1("i16"), 1.0, AluOpType.is_equal),
        "id0": lambda: cp(IDQ[0], V("id0"), V("idn"), scale=c1("m0")), "idk": lambda: cp(IDQ[1], V("idk"), V("idn"), scale=c1("m1")),
        "f1": lambda: ts(c1("f1"), c1("par"), -336.0, mul, 352.0, add), "f2": lambda: ts(c1("f2"), c1("i16"), 16.0, mul, c1("f1"), add),
        "ga": lambda: ts(c1("ga"), c1("par"), -208.0, mul, 224.0, add), "fa": lambda: ts(c1("fa"), c1("i16"), 16.0, mul, c1("ga"), add),
        "gb": lambda: ts(c1("gb"), c1("par"), -144.0, mul, 160.0, add), "fb": lambda: ts(c1("fb"), c1("i16"), 16.0, mul, c1("gb"), add),
        "f16": lambda: cp("v", c1("f16"), c1("i16")), "cw": lambda: ts(V("cw"), V("ik"), c1("f16"), add),
        "bc": lambda: ts(W("bs1", 0), V("ik"), c1("f16"), add, -float(HALF), add),
        "zP": lambda: fill(V("iP", 20, 32), 0), "zE": lambda: fill(V("iE", 20, 32), 0),
        "m2": lambda: ts(c1("m2"), c1("i16"), 2.0, AluOpType.is_equal, C + 15.0, mul), "mv": lambda: ts(c1("mv"), c1("m2"), 1.0, add),
    }

    def calls(r):
        R, N = str(r), str(r + 1)
        tu, yk, yg, bs, df, nbs, ndf, lp = "tu" + R, "yk" + R, "yg" + R, "bs" + R, "df" + R, "bs" + N, "df" + N, "lp" + N
        far, kl = partner[r - 1], V("kl" + R, 0, 10)
        hq, hs, lq, lsc = (V(n + R) for n in ("hq", "hs", "lq", "ls"))
        bank = {"n": 0, "f": 512}
        xq = lambda h: (V("xq", *RUN[h]), V("xs", *RUN[h]))
        score = lambda h: V("psA", bank[h], bank[h] + HALF)

        def made(h, t, a):
            o = 512 * t - min(RUN[h][0], C - 128)
            return V("psA" if h == "a" else "psB", o + a, o + RUN[h][1])

        seen = {}

        def again(n):
            seen[n] = seen.get(n, 0) + 1
            return r > 1 or seen[n] > 1

        def layer(h):
            a, b = min(RUN[h][0], C - 128), RUN[h][1]
            q, s = V("zq" + h, 0, b - a), V("zs" + h, 0, b - a)
            quant(q, s, V("zt", 4 * a, 4 * b))
            for t in PEORDER[h]:
                w = (128 * t, 128 * t + 128)
                mm(made(h, t, a), V("wq", *w), V("wp", *w), q, s)

        def leave():
            quant(hq, hs, V("hf"))
            send(far, lq, hq, "a_q" + R, 0, 16, codes=True)
            send(far, lsc, hs, "a_s" + R, 0, 16)

        def unpack():
            for t in range(4):
                e = (128 * t, 128 * t + 128)
                mm(V("psB", 512 * t, 512 * t + HALF), V("eq", *e), V("es", *e), lq, lsc)

        def product(h):
            u = "v" if r == 3 else "u"
            mm(score(h), V(u + "q"), V(u + "s"), *xq(h))

        def packed(h, queues):
            a, b = RUN[h]
            q, s = xq(h)
            store("y", T.oc[:, 4 * a:4 * b], q[0].bitcast(dt.uint8), q[1])
            for k in range(4):
                store(queues[k % 2], T.osc[4 * k:4 * k + 4, a:b], T.xs[32 * k:32 * k + 4, a:b], s[1])

        def result(h, q, dq):
            o = V("yo", *RUN[h])
            cp(q, o, score(h))
            store(dq, T.y[:, RUN[h][0]:RUN[h][1]], o[0], o[1])

        def lists():
            cp("s", V("pout", 0, C), P16("yb"), bias=float(HALF))
            cp("s", V("pout", C, 2 * C), pick(V("idn"), L(tu, 96)), bias=float(HALF))
            store("y", T.pl[:, :], T.pout[0:128:16, :], V("pout")[1])

        s = {
            "uP": lambda: cp("v", L("uP"), L("iP")), "uE": lambda: cp("v", L("uE"), L("iE")),
            "uF": lambda: cp("v", uF, L("iFY")), "uY": lambda: cp("v", uY, L("iFY", 20)),
            "sendP": lambda: send(far, L("lp1"), L("uP"), "a_p1", 0, 4),
            "po": lambda: cp("s", V("po"), pick(V("idn"), L("uP"))),
            "pE": lambda: cp("s", P16("cb"), pick(V("po"), L("uE"))),
            "iM": lambda: tt(L("iM"), L("iE"), L("cw"), AluOpType.min), "uM": lambda: cp("v", L("uM"), L("iM")),
            "bP": lambda: ts(W("bs1", 1), V("iP"), -float(HALF), add),
            "d0": lambda: tt(W("df1", 0), V("iE"), V("cw"), sub), "d1": lambda: tt(W("df1", 1), pick(V("tcb"), off(0)), W("bs1", 1), sub),
            "ya": lambda: tt(V("ya"), pick(V("id0"), uY), V("idk"), add),
            "wd": moved, "uFY": lambda: cp("v", V("uFY", 0, 40), V("iFY")), "off": lambda: ts(V("off", 0, 8), V("i8"), c1("f2"), add, 2.0 * C + 31, AluOpType.min),
            "ofa": lambda: ts(V("off", 8, 12), V("i8", 0, 4), c1("fa"), add, 415.0, AluOpType.min),
            "ofb": lambda: ts(V("off", 12, 16), V("i8", 0, 4), c1("fb"), add, 287.0, AluOpType.min),
            "c2": lambda: tt(W("tb", 2), pick(V("tnm"), off(2)), V("cw"), add), "k2": lambda: cp("v", W(tu, 2), W("tb", 2)),
            "p1": lambda: tt(W("pr", 1), pick(V("tnm"), off(1)), W(df, 1), mul),
            "b1": lambda: tt(W("tb", 1), W("pr", 1), W(bs, 1), add), "l1": lambda: ts(W(tu, 1), W("tb", 1), float(HALF), add),
            "pz": lambda: tt(W("pr", 0), pick(V("tnz"), off(0)), W(df, 0), mul),
            "bz": lambda: tt(W("tb", 0), W("pr", 0), W(bs, 0), add), "lz": lambda: ts(W(tu, 0), W("tb", 0), float(HALF), add),
            "yd": lambda: cp("s", V("yd"), pick(V("yc"), uF)),
            "uq": lambda: quant(V("uq"), V("us"), V("ut")), "vq": lambda: quant(V("vq"), V("vs"), V("vt")), "later": later,
            "p2": lambda: tt(W("pr", 2), pick(V("tnm"), off(2)), W("df1", 0), mul),
            "b2": lambda: tt(W("tb", 2), W("pr", 2), W("bs1", 0), add), "l2": lambda: ts(W(tu, 2), W("tb", 2), float(HALF), add),
            "p0": lambda: tt(W("pr", 0, 2), pick(V("tnm"), off(0, 2)), V(df), mul),
            "b0": lambda: tt(W("tb", 0, 2), W("pr", 0, 2), V(bs), add), "l0": lambda: ts(W(tu, 0, 2), W("tb", 0, 2), float(HALF), add),
            "p3": lambda: tt(W("pr", 3), pick(V("tnm"), off(3)), W(df, 1), mul),
            "b3": lambda: tt(W(nbs, 1), W("pr", 3), W(bs, 1), add), "l3": lambda: ts(W(tu, 3), W(nbs, 1), float(HALF), add),
            "sendB": lambda: send(partner[r], V(lp), W(tu, 3), "a_p" + N, 0, 8),
            "y3": lambda: wrapped(W("y31", 0, 2), "cc", 0, 2) if r == 1 else wrapped(W("y3" + R, 0), "cc", 0),
            "yf": lambda: cp("s", P16("yf"), pick(P16("yb"), uF)),
            "wY": lambda: wrapped(W(yk, 0), "yb", 0), "wK": lambda: wrapped(W(yk, 1), "yb", 1), "wG": lambda: wrapped(V(yg), "yf", 0),
            "sendK": lambda: send(far, kl, V(yk, 32, 42), "a_k" + R, *((8, 16) if r == 1 else (0, 8))),
            "qa": lambda: layer("a"), "qb": lambda: layer("b"), "hq": leave, "un": unpack,
            "cb": lambda: cp("s", P16("cb"), pick(V("cb", 0, C), L("uE"))),
            "cc": lambda: cp("s", P16("cc"), pick(P16("yb"), L("y31", 32)) if again("cc") else pick(V("yd"), uF)),
            "t2": lambda: cp("s", V("t2"), W("pr", 3), scale=-2.0), "dP": lambda: tt(W(ndf, 1), W(df, 1), V("t2"), add),
            "y3n": lambda: wrapped(W("y3" + N, 0), "cc", 0),
            "ua": lambda: cp("s", P16("ua"), pick(V("cb", 0, C), L("y3" + N))),
            "ub": lambda: cp("s", P16("ub"), pick(P16("cb"), L("y3" + N))),
            "nz": lambda: cp("s", P16("nz"), pick(P16("nm"), L("y3" + R))),
            "bF": lambda: cp("v", W(bs, 0), pick(V("tua"), off(0))),
            "dF": lambda: tt(W(df, 0), pick(V("tub"), off(0)), W(bs, 0), sub),
            "pads": pads,
            "on": lambda: packed("n", "yy"), "of": lambda: packed("f", "ys"), "pl": lists,
            "yn": lambda: result("n", "s", "y"), "yo": lambda: result("f", "v", "s"),
        }
        chain = {"g1": ("g1", 0, V("cb", 0, C if r == 1 else 2 * C + 16), tu, 64), "g2": ("g2", 0, V("g1"), tu, 32),
                 "g4": ("g4", 0, V("g2"), "lp1", 0), "g3": ("g3", 0, V("g4"), tu, 0),
                 "yb": ("yb", 16, V("g3"), "y31", 0) if r == 1 else ("yb", 16, V("g2"), tu, 0), "yh": ("yf", 16, P16("yb"), "uFY", 0),
                 "yc": ("yc", 0, V("ya"), "uFY", 0), "nz": ("nz", 16, P16("nm"), "y3" + R, 0)}

        def call(name):
            n, _, cut = name.partition(":")
            if n == "pq":
                return shared("cb", 0, V(WDST), lp if again(n) else "lp1", 0, int(cut))
            if n == "nm":
                o, i = V("nm", 16 + HALF, 16 + C), pick(V("sg"), V("uM", 10, 20))
                if r == 1:
                    ts(V("nm", 16, 16 + HALF), pick(V("sg"), V("uM", 0, 10)), 0.0, AluOpType.max)
                    return run("s", lambda: g.scalar.activation(o[0], i[0], ActivationFunctionType.Relu), [o], [i])
                ts(V("nm", 16, 16 + HALF), pick(V("sg"), V("uM", 0, 10)), 0.0, AluOpType.max, c1("mv"), mul)
                return run("s", lambda: g.scalar.activation(o[0], i[0], ActivationFunctionType.Relu, scale=c1("mv")[0]), [o], [i, c1("mv")])
            if n in constants:
                return constants[n]()
            if n in chain:
                return shared(*chain[n], int(cut) if cut else HALF)
            if n in s:
                return s[n]()
            if n[:2] in PADDED + LATER:
                return turn(n[:2], n[2:])
            if n[0] == "w" and len(n) == 3:
                return part(*{"Y": (yk, 0, "yb", 0), "K": (yk, 32, "yb", 1), "G": (yg, 0, "yf", 0)}[n[1]], n[2])
            if n[0] == "F":
                a, b = ((0, 224), (224, C))[int(n[1])]
                return cp(n[2], V("yf", 16 + a, 16 + b), pick(P16("yb"), V("uFY", a // 16, b // 16)))
            if n[1] in "nf":
                a, b = RUN[n[1]]
                if n[0] == "q":
                    return quant(*xq(n[1]), V("xi", 4 * a, 4 * b))
                if n[0] == "m":
                    return product(n[1])
                o, i = V("sg", a, b), score(n[1])
                if n[2] == "v":
                    return ts(o, i, 0.0, less)
                return run("s", lambda: g.scalar.activation(o[0], i[0], ActivationFunctionType.Sign, scale=-1.0), [o], [i])
            t = int(n[1])
            if n[0] == "e":
                e = (128 * t, 128 * t + 128)
                return quant(V("eq", *e), V("es", *e), V("et", 3 - t, 515 - t))
            if n[0] == "n":
                o = mixed("xi", t, HALF, C)
                return tt(o, pick(row("hg", t), V(yk, 42, 52)), o, add)
            if n[0] == "a":
                o = mixed("xi", t, 0, HALF)
                return tt(o, V("psB", 512 * t, 512 * t + HALF), o, add)
            if n[0] == "f":
                return cp(n[2], mixed("hf", t, 0, HALF), pick(row("hg", t), kl))
            a, b = RUN[n[2]]
            if n[0] == "X":
                return cp(n[3], row("xg", t, a, b), mixed("xi", t, a, b), scale=0.5)
            f = 0 if n[2] == "a" else 16
            if n[0] == "A":
                return cp(n[3:] or "s", row("ag", t, a, b), pick(row("xg", t), V(yk, f, f + (b - a) // 16)))
            if n[0] == "Z":
                return tt(mixed("zt", t, a, b), pick(row("xg", t), V(yg, f, f + (b - a) // 16)), row("ag", t, a, b), add)
            cp(n[3], row("hg", t, a, b), made(n[2], t, a), scale=0.03125)

        for name in ROUNDS[r - 1].split():
            call(name)

    for r in (1, 2, 3):
        calls(r)

    for s in LOADS:
        g.wait_ge(T.sem[s], 16)
    for s in ["c_g"] + ARRIVALS + ["sent", "c_t", "c_s", "c_v", "stored"]:
        g.wait_ge(T.sem[s], count[s])


PEORDER = {"a": (0, 2, 1, 3), "b": (0, 2, 1, 3)}
